import numpy as np
import ml_dtypes


def mxq(x, axis, fmt="e4m3"):
    dtype, down = {"e4m3": (ml_dtypes.float8_e4m3fn, 7), "e5m2": (ml_dtypes.float8_e5m2, 14)}[fmt]
    v = np.moveaxis(np.asarray(x, np.float32).astype(ml_dtypes.bfloat16).astype(np.float64), axis, -1)
    blocks = v.reshape(v.shape[:-1] + (-1, 32))
    amax = np.abs(blocks).max(-1, keepdims=True)
    byte = np.maximum(np.where(amax > 0, np.frexp(amax)[1] - 1 + 127, 0) - down, 1)
    scale = np.exp2(byte - 127.0)
    codes = (blocks / scale).astype(np.float32).astype(dtype).astype(np.float64)
    return np.moveaxis((codes * scale).reshape(v.shape), -1, axis)


WIDE = False


def mx_kscale(k):
    if not WIDE:
        return np.ones(k)
    levels = np.array([10, -10, 5, -5, 0])
    if k % 512:
        return np.exp2(np.random.permutation(np.resize(levels, k // 32))).repeat(32)
    a = np.empty((k // 512, 16))
    for p in range(k // 512):
        a[p, :8] = np.random.permutation(np.resize(levels, 8))
        for g in range(8):
            far = levels[np.abs(levels - a[p, g]) >= 10]
            a[p, g + 8] = far[np.random.randint(len(far))]
    return np.exp2(a.ravel()).repeat(32)


def f64(x):
    return np.asarray(x).astype(np.float64)


def striped(idx):
    return np.tile(idx.reshape(-1, 16).T, (8, 1)).astype(np.uint16)


def unstriped(offs):
    return offs[:16].T.reshape(-1).astype(np.int64)


def silu(v):
    return v / (1.0 + np.exp(-np.maximum(v, -700.0)))


K, T, S, J, H, N = 512, 4096, 1024, 512, 512, 128


def setup_inputs():
    n = np.random.standard_normal
    s = mx_kscale(K)[:, None]
    u = mx_kscale(H)
    r = mx_kscale(J)[:, None]
    return {
        "xT": (n((K, T)) * s).astype(np.float32),
        "eT": (n((J, S)) * r).astype(np.float32),
        "w1": (n((K, H)) / np.sqrt(K) / s * u).astype(np.float32),
        "w3": (n((J, H)) / np.sqrt(J) / r).astype(np.float32),
        "w2": (n((H, N)) / np.sqrt(H) / u[:, None]).astype(np.float32),
        "offs": striped(np.random.permutation(T)[:S]),
    }


def reference(xT, eT, w1, w3, w2, offs):
    c = mxq(f64(w1), 0, "e4m3").T @ mxq(f64(xT)[:, unstriped(offs)], 0, "e4m3")
    z = c * silu(mxq(f64(w3), 0, "e4m3").T @ mxq(f64(eT), 0, "e4m3"))
    return mxq(f64(w2), 0, "e4m3").T @ mxq(z, 0, "e4m3")

@@ -1,0 +1,282 @@
+from contextlib import ExitStack
+
+import concourse.mybir as mybir
+
+F32 = mybir.dt.float32
+BF16 = mybir.dt.bfloat16
+U32 = mybir.dt.uint32
+U16 = mybir.dt.uint16
+U8 = mybir.dt.uint8
+FP8X4 = mybir.dt.float8_e4m3fn_x4
+SILU = mybir.ActivationFunctionType.Silu
+MULT = mybir.AluOpType.mult
+ADD = mybir.AluOpType.add
+
+P = 128
+T, S, H, N = 4096, 1024, 512, 128
+FLOPS = 2 * 512 * H * S * 2 + 2 * H * N * S
+HALF = 512
+CH = 256
+U = 128
+
+
+def tile_picked_schnet_silu_e_kernel(tc, xT, eT, w1, w3, w2, offs, out):
+    nc = tc.nc
+    with ExitStack() as ctx:
+        keep = ctx.enter_context(tc.tile_pool(name="keep", bufs=1))
+        ring = ctx.enter_context(tc.tile_pool(name="ring", bufs=3))
+        psum = ctx.enter_context(tc.psum_pool(name="psum", bufs=3))
+
+        offsets = keep.tile([P, S // 16], U16, name="offsets")
+        x_rows = xT.rearrange("(p t) n -> p t n", t=4)
+        e_rows = eT.rearrange("(p j) n -> p j n", j=4)
+        planes = [keep.tile([P, T], F32, name=f"plane{t}") for t in range(4)]
+        raw = {}
+        raw["w1"] = keep.tile([P, 4, H], F32, name="w1_raw")
+        raw["w3"] = keep.tile([P, 4, H], F32, name="w3_raw")
+        raw["w2"] = keep.tile([P, 4, N], F32, name="w2_raw")
+        e_raw = [keep.tile([P, 4, CH], F32, name=f"e_raw{k}") for k in range(S // CH)]
+
+        for what in ["x0","x1","x2","x3","w1","w3","e0","e1","e2","w2","e3"]:
+            if what[0] == "x":
+                t = int(what[1])
+                nc.sync.dma_start(out=planes[t][:], in_=x_rows[:, t, :])
+                if t == 0:
+                    nc.sync.dma_start(offsets[:], offs)
+            elif what == "w1":
+                nc.sync.dma_start(out=raw["w1"][:], in_=w1.rearrange("(p j) c -> p j c", j=4))
+            elif what == "w3":
+                nc.sync.dma_start(out=raw["w3"][:], in_=w3.rearrange("(p j) c -> p j c", j=4))
+            elif what == "w2":
+                nc.sync.dma_start(out=raw["w2"][:], in_=w2.rearrange("(p j) c -> p j c", j=4))
+            else:
+                k = int(what[1])
+                nc.sync.dma_start(out=e_raw[k][:], in_=e_rows[:, :, k * CH : (k + 1) * CH])
+
+        warm = keep.tile([P, 1], F32, name="warm")
+        nc.vector.memset(warm[:], 0.0)
+        nc.scalar.activation(out=warm[:], in_=warm[:], func=SILU)
+
+        def copy_on(engine, dst, src):
+            if engine == "S":
+                nc.scalar.copy(out=dst, in_=src)
+            elif engine == "V":
+                nc.vector.tensor_copy(out=dst, in_=src)
+            else:
+                nc.gpsimd.tensor_scalar(out=dst, in0=src, scalar1=1.0, scalar2=0.0, op0=MULT, op1=ADD)
+
+        codes = {}
+        scales = {}
+        grouped = {}
+
+        def new_w(name):
+            grouped[name] = keep.tile([P, raw[name].shape[2] * 4], BF16, align_bytes=64, name=f"{name}_grouped")
+
+        def interleave_w2(engine):
+            new_w("w2")
+            copy_on(
+                engine,
+                grouped["w2"][:].rearrange("p (c i j) -> p c j i", i=4, j=4),
+                raw["w2"][:].rearrange("p j (c i) -> p c j i", i=4),
+            )
+
+        def interleave_w(name, engine, t0, t1):
+            copy_on(
+                engine,
+                grouped[name][:].rearrange("p (t m j) -> p m t j", t=4, j=4)[:, :, t0:t1, :],
+                raw[name][:].rearrange("p j (m t) -> p m t j", t=4)[:, :, t0:t1, :],
+            )
+
+        def quantize(name, width):
+            c = keep.tile([P, width], U32, align_bytes=64, name=f"{name}_codes")
+            s = keep.tile([P, width], U8, align_bytes=64, name=f"{name}_scales")
+            codes[name] = c
+            scales[name] = s
+            nc.vector.quantize_mx(out=c[:].bitcast(FP8X4), scales=s[:], in_=grouped[name][:])
+
+        def interleave_e(k, engine):
+            g = keep.tile([P, CH * 4], BF16, align_bytes=64, name=f"e{k}_grouped")
+            grouped[f"e{k}"] = g
+            copy_on(
+                engine,
+                g[:].rearrange("p (c i j) -> p c j i", i=4, j=4),
+                e_raw[k][:].rearrange("p j (c i) -> p c j i", i=4),
+            )
+
+        x_grouped = [keep.tile([P, HALF, 4], BF16, align_bytes=64, name=f"x{h}_grouped") for h in range(2)]
+
+        def gather(t, h):
+            nc.vector.tensor_copy(
+                x_grouped[h][:, :, t], planes[t][:].indirect(offsets[:, h * HALF // 16 : (h + 1) * HALF // 16])
+            )
+
+        def quantize_x(h):
+            c = keep.tile([P, HALF], U32, align_bytes=64, name=f"x{h}_codes")
+            s = keep.tile([P, HALF], U8, align_bytes=64, name=f"x{h}_scales")
+            codes[f"x{h}"] = c
+            scales[f"x{h}"] = s
+            nc.vector.quantize_mx(
+                out=c[:].bitcast(FP8X4), scales=s[:], in_=x_grouped[h][:].rearrange("p n j -> p (n j)")
+            )
+
+        def product(w, x, c0, acc):
+            for t in range(4):
+                nc.tensor.matmul_mx(
+                    out=acc[:, t, :],
+                    lhsT=codes[w][:, t * P : (t + 1) * P].bitcast(FP8X4),
+                    lhsT_scale=scales[w][:, t * P : (t + 1) * P],
+                    rhs=codes[x][:, c0 : c0 + U].bitcast(FP8X4),
+                    rhs_scale=scales[x][:, c0 : c0 + U],
+                    start=True,
+                    stop=True,
+                )
+
+        filt = {}
+        cacc = {}
+        facc = {}
+        oacc = {}
+        zc_tiles = {}
+        z_tiles = {}
+
+        def f_unit(u):
+            acc = psum.tile([P, 4, U], F32, name="f_acc")
+            product("w3", f"e{u * U // CH}", u * U % CH, acc)
+            facc[u] = acc
+
+        def silu(u):
+            s = ring.tile([P, U, 4], F32, name="filter", bufs=8)
+            filt[u] = s
+            nc.scalar.activation(out=s[:], in_=facc[u][:].rearrange("p t n -> p n t"), func=SILU)
+
+        def c_unit(u):
+            acc = psum.tile([P, 4, U], F32, name="c_acc")
+            cacc[u] = acc
+            product("w1", f"x{u * U // HALF}", u * U % HALF, acc)
+
+        def mult(u, z, col):
+            nc.vector.tensor_tensor(
+                out=z[:, col * 4 : (col + U) * 4].rearrange("p (n t) -> p n t", t=4),
+                in0=cacc[u][:].rearrange("p t n -> p n t"),
+                in1=filt[u][:],
+                op=MULT,
+            )
+
+        def mult_g(u, z, col):
+            cs = ring.tile([P, U, 4], F32, name="c_sbuf", bufs=4)
+            nc.scalar.copy(out=cs[:], in_=cacc[u][:].rearrange("p t n -> p n t"))
+            nc.gpsimd.tensor_tensor(
+                out=z[:, col * 4 : (col + U) * 4].rearrange("p (n t) -> p n t", t=4), in0=cs[:], in1=filt[u][:], op=MULT
+            )
+
+        def new_z(g):
+            n = len(g) * U
+            z_tiles[g[0]] = keep.tile([P, n * 4], BF16, align_bytes=64, name=f"z{g[0]}")
+
+        def quantize_z(g):
+            n = len(g) * U
+            zc = keep.tile([P, n], U32, align_bytes=64, name=f"z{g[0]}_codes")
+            zs = keep.tile([P, n], U8, align_bytes=64, name=f"z{g[0]}_scales")
+            nc.vector.quantize_mx(out=zc[:].bitcast(FP8X4), scales=zs[:], in_=z_tiles[g[0]][:])
+            zc_tiles[g[0]] = (zc, zs)
+
+        def project(g):
+            zc, zs = zc_tiles[g[0]]
+            acc = psum.tile([P, len(g) * U], F32, name="o_acc", bufs=2)
+            oacc[g[0]] = acc
+            nc.tensor.matmul_mx(
+                out=acc[:],
+                lhsT=codes["w2"][:].bitcast(FP8X4),
+                lhsT_scale=scales["w2"][:],
+                rhs=zc[:].bitcast(FP8X4),
+                rhs_scale=zs[:],
+                start=True,
+                stop=True,
+            )
+
+        def store(g, engine):
+            n = len(g) * U
+            acc = oacc[g[0]]
+            y = keep.tile([P, n], F32, name=f"y{g[0]}")
+            copy_on(engine, y[:], acc[:])
+            nc.sync.dma_start(out=out[:, g[0] * U : g[0] * U + n], in_=y[:])
+
+        gather(0, 0)
+        gather(0, 1)
+        gather(1, 0)
+        gather(1, 1)
+        gather(2, 0)
+        gather(2, 1)
+        gather(3, 0)
+        gather(3, 1)
+        new_w("w1")
+        interleave_w("w1", "G", 2, 4)
+        interleave_w("w1", "S", 0, 2)
+        quantize_x(0)
+        quantize_x(1)
+        quantize("w1", 512)
+        new_w("w3")
+        interleave_w("w3", "S", 0, 2)
+        c_unit(0)
+        c_unit(1)
+        c_unit(2)
+        interleave_w("w3", "S", 2, 4)
+        interleave_e(0, "V")
+        quantize("e0", CH)
+        quantize("w3", 512)
+        interleave_e(1, "S")
+        f_unit(0)
+        f_unit(1)
+        silu(0)
+        quantize("e1", CH)
+        interleave_e(2, "V")
+        f_unit(2)
+        silu(1)
+        interleave_w2("G")
+        f_unit(3)
+        new_z([0, 1])
+        mult(0, z_tiles[0], 0 * U)
+        silu(2)
+        quantize("e2", CH)
+        silu(3)
+        c_unit(3)
+        mult(1, z_tiles[0], 1 * U)
+        f_unit(4)
+        interleave_e(3, "S")
+        f_unit(5)
+        quantize("w2", 128)
+        quantize_z([0, 1])
+        c_unit(4)
+        new_z([2, 3])
+        mult(2, z_tiles[2], 0 * U)
+        project([0, 1])
+        silu(4)
+        quantize("e3", CH)
+        c_unit(5)
+        store([0, 1], "S")
+        mult(3, z_tiles[2], 1 * U)
+        f_unit(6)
+        silu(5)
+        f_unit(7)
+        new_z([4, 5])
+        mult(4, z_tiles[4], 0 * U)
+        silu(6)
+        c_unit(6)
+        quantize_z([2, 3])
+        c_unit(7)
+        silu(7)
+        mult(5, z_tiles[4], 1 * U)
+        project([2, 3])
+        store([2, 3], "S")
+        new_z([6])
+        mult(6, z_tiles[6], 0 * U)
+        quantize_z([4, 5])
+        new_z([7])
+        mult(7, z_tiles[7], 0 * U)
+        project([4, 5])
+        store([4, 5], "S")
+        quantize_z([6])
+        quantize_z([7])
+        project([6])
+        store([6], "S")
+        project([7])
+        store([7], "S")

@@ -9,14 +9,13 @@ U16 = mybir.dt.uint16
 U8 = mybir.dt.uint8
 FP8X4 = mybir.dt.float8_e4m3fn_x4
 SILU = mybir.ActivationFunctionType.Silu
+COPY = mybir.ActivationFunctionType.Copy
 MULT = mybir.AluOpType.mult
-ADD = mybir.AluOpType.add
 
 P = 128
 T, S, H, N = 4096, 1024, 512, 128
 FLOPS = 2 * 512 * H * S * 2 + 2 * H * N * S
 HALF = 512
-CH = 256
 U = 128
 
 
@@ -24,7 +23,6 @@ def tile_picked_schnet_silu_e_kernel(tc, xT, eT, w1, w3, w2, offs, out):
     nc = tc.nc
     with ExitStack() as ctx:
         keep = ctx.enter_context(tc.tile_pool(name="keep", bufs=1))
-        ring = ctx.enter_context(tc.tile_pool(name="ring", bufs=3))
         psum = ctx.enter_context(tc.psum_pool(name="psum", bufs=3))
 
         offsets = keep.tile([P, S // 16], U16, name="offsets")
@@ -35,89 +33,77 @@ def tile_picked_schnet_silu_e_kernel(tc, xT, eT, w1, w3, w2, offs, out):
         raw["w1"] = keep.tile([P, 4, H], F32, name="w1_raw")
         raw["w3"] = keep.tile([P, 4, H], F32, name="w3_raw")
         raw["w2"] = keep.tile([P, 4, N], F32, name="w2_raw")
-        e_raw = [keep.tile([P, 4, CH], F32, name=f"e_raw{k}") for k in range(S // CH)]
+        e_cols = {}
+        grouped = {}
+        windows = {}
 
-        for what in ["x0","x1","x2","x3","w1","w3","e0","e1","e2","w2","e3"]:
-            if what[0] == "x":
-                t = int(what[1])
-                nc.sync.dma_start(out=planes[t][:], in_=x_rows[:, t, :])
-                if t == 0:
-                    nc.sync.dma_start(offsets[:], offs)
-            elif what == "w1":
-                nc.sync.dma_start(out=raw["w1"][:], in_=w1.rearrange("(p j) c -> p j c", j=4))
-            elif what == "w3":
-                nc.sync.dma_start(out=raw["w3"][:], in_=w3.rearrange("(p j) c -> p j c", j=4))
-            elif what == "w2":
-                nc.sync.dma_start(out=raw["w2"][:], in_=w2.rearrange("(p j) c -> p j c", j=4))
-            else:
-                k = int(what[1])
-                nc.sync.dma_start(out=e_raw[k][:], in_=e_rows[:, :, k * CH : (k + 1) * CH])
+        def load_x(t, c0=0, c1=T):
+            nc.sync.dma_start(out=planes[t][:, c0:c1], in_=x_rows[:, t, c0:c1])
 
-        warm = keep.tile([P, 1], F32, name="warm")
-        nc.vector.memset(warm[:], 0.0)
-        nc.scalar.activation(out=warm[:], in_=warm[:], func=SILU)
+        def load_w(name, w):
+            nc.sync.dma_start(out=raw[name][:], in_=w.rearrange("(p j) c -> p j c", j=4))
 
-        def copy_on(engine, dst, src):
-            if engine == "S":
-                nc.scalar.copy(out=dst, in_=src)
-            elif engine == "V":
-                nc.vector.tensor_copy(out=dst, in_=src)
-            else:
-                nc.gpsimd.tensor_scalar(out=dst, in0=src, scalar1=1.0, scalar2=0.0, op0=MULT, op1=ADD)
+        def load_offs():
+            nc.sync.dma_start(offsets[:], offs)
 
+        def load_e(k, c0, c1):
+            e_cols[k] = (c0, c1)
+            raw[f"e{k}"] = keep.tile([P, 4, c1 - c0], F32, name=f"e_raw{k}")
+            grouped[f"e{k}"] = keep.tile([P, (c1 - c0) * 4], BF16, align_bytes=64, name=f"e{k}_grouped")
+            nc.sync.dma_start(out=raw[f"e{k}"][:], in_=e_rows[:, :, c0:c1])
+
+        def load_w2():
+            rows = w2.rearrange("(q t i) c -> i q t c", t=4, i=4)
+            for i in range(4):
+                nc.sync.dma_start(out=raw["w2"][i:P:4, :, :], in_=rows[i])
+
+        copy_on = {"S": nc.scalar.copy, "V": nc.vector.tensor_copy}
         codes = {}
         scales = {}
-        grouped = {}
-
-        def new_w(name):
+        for name in ("w1", "w3", "w2"):
             grouped[name] = keep.tile([P, raw[name].shape[2] * 4], BF16, align_bytes=64, name=f"{name}_grouped")
-
-        def interleave_w2(engine):
-            new_w("w2")
-            copy_on(
-                engine,
-                grouped["w2"][:].rearrange("p (c i j) -> p c j i", i=4, j=4),
-                raw["w2"][:].rearrange("p j (c i) -> p c j i", i=4),
-            )
-
-        def interleave_w(name, engine, t0, t1):
-            copy_on(
-                engine,
-                grouped[name][:].rearrange("p (t m j) -> p m t j", t=4, j=4)[:, :, t0:t1, :],
-                raw[name][:].rearrange("p j (m t) -> p m t j", t=4)[:, :, t0:t1, :],
-            )
-
-        def quantize(name, width):
-            c = keep.tile([P, width], U32, align_bytes=64, name=f"{name}_codes")
-            s = keep.tile([P, width], U8, align_bytes=64, name=f"{name}_scales")
-            codes[name] = c
-            scales[name] = s
-            nc.vector.quantize_mx(out=c[:].bitcast(FP8X4), scales=s[:], in_=grouped[name][:])
-
-        def interleave_e(k, engine):
-            g = keep.tile([P, CH * 4], BF16, align_bytes=64, name=f"e{k}_grouped")
-            grouped[f"e{k}"] = g
-            copy_on(
-                engine,
-                g[:].rearrange("p (c i j) -> p c j i", i=4, j=4),
-                e_raw[k][:].rearrange("p j (c i) -> p c j i", i=4),
-            )
-
         x_grouped = [keep.tile([P, HALF, 4], BF16, align_bytes=64, name=f"x{h}_grouped") for h in range(2)]
+
+        def interleave(name, engine, c0=0, c1=None):
+            copy_on[engine](
+                out=grouped[name][:].rearrange("p (c i j) -> p c j i", i=4, j=4)[:, c0:c1],
+                in_=raw[name][:].rearrange("p j (c i) -> p c j i", i=4)[:, c0:c1],
+            )
+
+        def interleave_w(name, engine, q0, q1):
+            copy_on[engine](
+                out=grouped[name][:].rearrange("p (t q i j) -> p q t j i", t=4, i=4, j=4)[:, q0:q1],
+                in_=raw[name][:].rearrange("p j (q t i) -> p q t j i", t=4, i=4)[:, q0:q1],
+            )
+
+        def quantize(name, source):
+            width = source.shape[1] // 4
+            codes[name] = keep.tile([P, width], U32, align_bytes=64, name=f"{name}_codes")
+            scales[name] = keep.tile([P, width], U8, align_bytes=64, name=f"{name}_scales")
+            nc.vector.quantize_mx(out=codes[name][:].bitcast(FP8X4), scales=scales[name][:], in_=source)
+
+        def quantize_in(name):
+            quantize(name, grouped[name][:])
 
         def gather(t, h):
             nc.vector.tensor_copy(
                 x_grouped[h][:, :, t], planes[t][:].indirect(offsets[:, h * HALF // 16 : (h + 1) * HALF // 16])
             )
 
-        def quantize_x(h):
-            c = keep.tile([P, HALF], U32, align_bytes=64, name=f"x{h}_codes")
-            s = keep.tile([P, HALF], U8, align_bytes=64, name=f"x{h}_scales")
-            codes[f"x{h}"] = c
-            scales[f"x{h}"] = s
-            nc.vector.quantize_mx(
-                out=c[:].bitcast(FP8X4), scales=s[:], in_=x_grouped[h][:].rearrange("p n j -> p (n j)")
+        def cast(t, c0, c1, engine):
+            if t not in windows:
+                windows[t] = keep.tile([P, T], BF16, name=f"window{t}")
+            copy_on[engine](out=windows[t][:, c0:c1], in_=planes[t][:, c0:c1])
+
+        def gather_s(t, h):
+            nc.scalar.activation(
+                out=x_grouped[h][:, :, t],
+                in_=windows[t][:].indirect(offsets[:, h * HALF // 16 : (h + 1) * HALF // 16]),
+                func=COPY,
             )
+
+        def quantize_x(h):
+            quantize(f"x{h}", x_grouped[h][:].rearrange("p n j -> p (n j)"))
 
         def product(w, x, c0, acc):
             for t in range(4):
@@ -135,148 +121,136 @@ def tile_picked_schnet_silu_e_kernel(tc, xT, eT, w1, w3, w2, offs, out):
         cacc = {}
         facc = {}
         oacc = {}
-        zc_tiles = {}
         z_tiles = {}
 
         def f_unit(u):
-            acc = psum.tile([P, 4, U], F32, name="f_acc")
-            product("w3", f"e{u * U // CH}", u * U % CH, acc)
-            facc[u] = acc
+            facc[u] = psum.tile([P, 4, U], F32, name="f_acc")
+            k = [k for k in e_cols if e_cols[k][0] <= u * U < e_cols[k][1]][0]
+            product("w3", f"e{k}", u * U - e_cols[k][0], facc[u])
 
         def silu(u):
-            s = ring.tile([P, U, 4], F32, name="filter", bufs=8)
-            filt[u] = s
-            nc.scalar.activation(out=s[:], in_=facc[u][:].rearrange("p t n -> p n t"), func=SILU)
+            filt[u] = keep.tile([P, U, 4], F32, name=f"filter{u}")
+            nc.scalar.activation(out=filt[u][:], in_=facc[u][:].rearrange("p t n -> p n t"), func=SILU)
 
         def c_unit(u):
-            acc = psum.tile([P, 4, U], F32, name="c_acc")
-            cacc[u] = acc
-            product("w1", f"x{u * U // HALF}", u * U % HALF, acc)
+            cacc[u] = psum.tile([P, 4, U], F32, name="c_acc")
+            product("w1", f"x{u * U // HALF}", u * U % HALF, cacc[u])
 
-        def mult(u, z, col):
+        def mult(u, g):
+            if u == g[0]:
+                z_tiles[g[0]] = keep.tile([P, len(g) * U * 4], BF16, align_bytes=64, name=f"z{g[0]}")
+            col = (u - g[0]) * U
             nc.vector.tensor_tensor(
-                out=z[:, col * 4 : (col + U) * 4].rearrange("p (n t) -> p n t", t=4),
+                out=z_tiles[g[0]][:, col * 4 : (col + U) * 4].rearrange("p (n t) -> p n t", t=4),
                 in0=cacc[u][:].rearrange("p t n -> p n t"),
                 in1=filt[u][:],
                 op=MULT,
             )
 
-        def mult_g(u, z, col):
-            cs = ring.tile([P, U, 4], F32, name="c_sbuf", bufs=4)
-            nc.scalar.copy(out=cs[:], in_=cacc[u][:].rearrange("p t n -> p n t"))
-            nc.gpsimd.tensor_tensor(
-                out=z[:, col * 4 : (col + U) * 4].rearrange("p (n t) -> p n t", t=4), in0=cs[:], in1=filt[u][:], op=MULT
-            )
-
-        def new_z(g):
-            n = len(g) * U
-            z_tiles[g[0]] = keep.tile([P, n * 4], BF16, align_bytes=64, name=f"z{g[0]}")
-
         def quantize_z(g):
-            n = len(g) * U
-            zc = keep.tile([P, n], U32, align_bytes=64, name=f"z{g[0]}_codes")
-            zs = keep.tile([P, n], U8, align_bytes=64, name=f"z{g[0]}_scales")
-            nc.vector.quantize_mx(out=zc[:].bitcast(FP8X4), scales=zs[:], in_=z_tiles[g[0]][:])
-            zc_tiles[g[0]] = (zc, zs)
+            quantize(f"z{g[0]}", z_tiles[g[0]][:])
 
         def project(g):
-            zc, zs = zc_tiles[g[0]]
-            acc = psum.tile([P, len(g) * U], F32, name="o_acc", bufs=2)
-            oacc[g[0]] = acc
+            oacc[g[0]] = psum.tile([P, len(g) * U], F32, name="o_acc", bufs=2)
             nc.tensor.matmul_mx(
-                out=acc[:],
+                out=oacc[g[0]][:],
                 lhsT=codes["w2"][:].bitcast(FP8X4),
                 lhsT_scale=scales["w2"][:],
-                rhs=zc[:].bitcast(FP8X4),
-                rhs_scale=zs[:],
+                rhs=codes[f"z{g[0]}"][:].bitcast(FP8X4),
+                rhs_scale=scales[f"z{g[0]}"][:],
                 start=True,
                 stop=True,
             )
 
         def store(g, engine):
             n = len(g) * U
-            acc = oacc[g[0]]
             y = keep.tile([P, n], F32, name=f"y{g[0]}")
-            copy_on(engine, y[:], acc[:])
+            copy_on[engine](out=y[:], in_=oacc[g[0]][:])
             nc.sync.dma_start(out=out[:, g[0] * U : g[0] * U + n], in_=y[:])
 
-        gather(0, 0)
-        gather(0, 1)
-        gather(1, 0)
-        gather(1, 1)
-        gather(2, 0)
-        gather(2, 1)
-        gather(3, 0)
-        gather(3, 1)
-        new_w("w1")
-        interleave_w("w1", "G", 2, 4)
-        interleave_w("w1", "S", 0, 2)
+        def warm():
+            w = keep.tile([P, 1], F32, name="warm")
+            nc.vector.memset(w[:], 0.0)
+            nc.scalar.activation(out=w[:], in_=w[:], func=SILU)
+
+        load_x(0)
+        load_offs()
+        load_x(1)
+        load_x(2)
+        load_x(3)
+        load_w("w3", w3)
+        load_e(0,0,256)
+        load_w("w1", w1)
+        load_e(1,256,512)
+        load_e(2,512,768)
+        load_e(3,768,1024)
+        load_w2()
+        warm()
+        for t in range(4):
+            gather(t, 0)
+            gather(t, 1)
+        interleave_w("w3", "S", 0, 32)
         quantize_x(0)
         quantize_x(1)
-        quantize("w1", 512)
-        new_w("w3")
-        interleave_w("w3", "S", 0, 2)
+        interleave("e0", "S")
+        quantize_in("w3")
+        quantize_in("e0")
+        interleave_w("w1", "S", 0, 12)
+        interleave_w("w1", "V", 12, 32)
+        f_unit(0)
+        f_unit(1)
+        quantize_in("w1")
+        silu(0)
+        silu(1)
         c_unit(0)
         c_unit(1)
         c_unit(2)
-        interleave_w("w3", "S", 2, 4)
-        interleave_e(0, "V")
-        quantize("e0", CH)
-        quantize("w3", 512)
-        interleave_e(1, "S")
-        f_unit(0)
-        f_unit(1)
-        silu(0)
-        quantize("e1", CH)
-        interleave_e(2, "V")
+        interleave("e1", "V")
+        interleave("e2", "S")
+        mult(0, [0, 1])
+        quantize_in("e1")
         f_unit(2)
-        silu(1)
-        interleave_w2("G")
         f_unit(3)
-        new_z([0, 1])
-        mult(0, z_tiles[0], 0 * U)
-        silu(2)
-        quantize("e2", CH)
-        silu(3)
         c_unit(3)
-        mult(1, z_tiles[0], 1 * U)
+        mult(1, [0, 1])
+        quantize_in("e2")
         f_unit(4)
-        interleave_e(3, "S")
-        f_unit(5)
-        quantize("w2", 128)
-        quantize_z([0, 1])
         c_unit(4)
-        new_z([2, 3])
-        mult(2, z_tiles[2], 0 * U)
-        project([0, 1])
-        silu(4)
-        quantize("e3", CH)
+        silu(2)
+        quantize_z([0, 1])
+        interleave("e3", "V", 0, 32)
+        silu(3)
+        f_unit(5)
+        interleave("e3", "S", 32, 64)
+        mult(2, [2, 3])
         c_unit(5)
-        store([0, 1], "S")
-        mult(3, z_tiles[2], 1 * U)
+        mult(3, [2, 3])
+        c_unit(6)
+        silu(4)
+        quantize_in("e3")
         f_unit(6)
         silu(5)
         f_unit(7)
-        new_z([4, 5])
-        mult(4, z_tiles[4], 0 * U)
-        silu(6)
-        c_unit(6)
-        quantize_z([2, 3])
+        mult(4, [4, 5])
         c_unit(7)
-        silu(7)
-        mult(5, z_tiles[4], 1 * U)
+        interleave("w2", "S")
+        quantize_z([2, 3])
+        mult(5, [4, 5])
+        silu(6)
+        quantize_in("w2")
+        project([0, 1])
         project([2, 3])
-        store([2, 3], "S")
-        new_z([6])
-        mult(6, z_tiles[6], 0 * U)
+        silu(7)
+        mult(6, [6])
         quantize_z([4, 5])
-        new_z([7])
-        mult(7, z_tiles[7], 0 * U)
+        store([0, 1], "S")
+        store([2, 3], "S")
+        mult(7, [7])
         project([4, 5])
-        store([4, 5], "S")
         quantize_z([6])
+        store([4, 5], "S")
         quantize_z([7])
         project([6])
         store([6], "S")
         project([7])
-        store([7], "S")
+        store([7], "V")

@@ -53,9 +53,9 @@ def tile_picked_schnet_silu_e_kernel(tc, xT, eT, w1, w3, w2, offs, out):
             nc.sync.dma_start(out=raw[f"e{k}"][:], in_=e_rows[:, :, c0:c1])
 
         def load_w2():
-            rows = w2.rearrange("(q t i) c -> i q t c", t=4, i=4)
-            for i in range(4):
-                nc.sync.dma_start(out=raw["w2"][i:P:4, :, :], in_=rows[i])
+            rows = w2.rearrange("(q t i) c -> i q t c", t=4, i=2)
+            for i in range(2):
+                nc.sync.dma_start(out=raw["w2"][i:P:2, :, :], in_=rows[i])
 
         copy_on = {"S": nc.scalar.copy, "V": nc.vector.tensor_copy}
         codes = {}
@@ -72,8 +72,24 @@ def tile_picked_schnet_silu_e_kernel(tc, xT, eT, w1, w3, w2, offs, out):
 
         def interleave_w(name, engine, q0, q1):
             copy_on[engine](
-                out=grouped[name][:].rearrange("p (t q i j) -> p q t j i", t=4, i=4, j=4)[:, q0:q1],
-                in_=raw[name][:].rearrange("p j (q t i) -> p q t j i", t=4, i=4)[:, q0:q1],
+                out=grouped[name][:].rearrange("p (t q i j) -> p q t j i", t=4, i=2, j=4)[:, 2 * q0 : 2 * q1],
+                in_=raw[name][:].rearrange("p j (q t i) -> p q t j i", t=4, i=2)[:, 2 * q0 : 2 * q1],
+            )
+
+        def interleave_t(name, engine, t0, t1, q0=0, q1=32):
+            copy_on[engine](
+                out=grouped[name][:].rearrange("p (t q i j) -> p q t j i", t=4, i=2, j=4)[:, 2 * q0 : 2 * q1, t0:t1],
+                in_=raw[name][:].rearrange("p j (q t i) -> p q t j i", t=4, i=2)[:, 2 * q0 : 2 * q1, t0:t1],
+            )
+
+        def quantize_t(name, t0, t1):
+            if name not in codes:
+                codes[name] = keep.tile([P, H], U32, align_bytes=64, name=f"{name}_codes")
+                scales[name] = keep.tile([P, H], U8, align_bytes=64, name=f"{name}_scales")
+            nc.vector.quantize_mx(
+                out=codes[name][:, t0 * P : t1 * P].bitcast(FP8X4),
+                scales=scales[name][:, t0 * P : t1 * P],
+                in_=grouped[name][:, t0 * 4 * P : t1 * 4 * P],
             )
 
         def quantize(name, source):
@@ -105,8 +121,8 @@ def tile_picked_schnet_silu_e_kernel(tc, xT, eT, w1, w3, w2, offs, out):
         def quantize_x(h):
             quantize(f"x{h}", x_grouped[h][:].rearrange("p n j -> p (n j)"))
 
-        def product(w, x, c0, acc):
-            for t in range(4):
+        def product(w, x, c0, acc, order=(0, 1, 2, 3)):
+            for t in order:
                 nc.tensor.matmul_mx(
                     out=acc[:, t, :],
                     lhsT=codes[w][:, t * P : (t + 1) * P].bitcast(FP8X4),
@@ -135,6 +151,10 @@ def tile_picked_schnet_silu_e_kernel(tc, xT, eT, w1, w3, w2, offs, out):
         def c_unit(u):
             cacc[u] = psum.tile([P, 4, U], F32, name="c_acc")
             product("w1", f"x{u * U // HALF}", u * U % HALF, cacc[u])
+
+        def c_unit_t(u, order):
+            cacc[u] = psum.tile([P, 4, U], F32, name="c_acc")
+            product("w1", f"x{u * U // HALF}", u * U % HALF, cacc[u], order)
 
         def mult(u, g):
             if u == g[0]:
@@ -173,6 +193,7 @@ def tile_picked_schnet_silu_e_kernel(tc, xT, eT, w1, w3, w2, offs, out):
             nc.vector.memset(w[:], 0.0)
             nc.scalar.activation(out=w[:], in_=w[:], func=SILU)
 
+        ORD = (3, 0, 1, 2)
         load_x(0)
         load_offs()
         load_x(1)
@@ -191,50 +212,57 @@ def tile_picked_schnet_silu_e_kernel(tc, xT, eT, w1, w3, w2, offs, out):
             gather(t, 1)
         interleave_w("w3", "S", 0, 32)
         quantize_x(0)
+        interleave("e0", "V", 0, 32)
+        interleave("e0", "S", 32, 64)
         quantize_x(1)
-        interleave("e0", "S")
         quantize_in("w3")
         quantize_in("e0")
-        interleave_w("w1", "S", 0, 12)
-        interleave_w("w1", "V", 12, 32)
+        interleave_t("w1", "S", 3, 4)
+        interleave_t("w1", "V", 0, 2)
+        interleave_t("w1", "V", 2, 3, 0, 16)
+        interleave_t("w1", "S", 2, 3, 16, 32)
         f_unit(0)
         f_unit(1)
-        quantize_in("w1")
+        quantize_t("w1", 3, 4)
+        quantize_t("w1", 0, 2)
+        quantize_t("w1", 2, 3)
         silu(0)
+        c_unit_t(0, ORD)
+        c_unit_t(1, ORD)
+        c_unit_t(2, ORD)
+        interleave("e1", "V", 0, 32)
+        interleave("e1", "S", 32, 64)
         silu(1)
-        c_unit(0)
-        c_unit(1)
-        c_unit(2)
-        interleave("e1", "V")
-        interleave("e2", "S")
         mult(0, [0, 1])
         quantize_in("e1")
         f_unit(2)
         f_unit(3)
-        c_unit(3)
+        c_unit_t(3, ORD)
+        interleave("e2", "S", 32, 64)
         mult(1, [0, 1])
-        quantize_in("e2")
-        f_unit(4)
-        c_unit(4)
+        c_unit_t(4, ORD)
+        interleave("e2", "V", 0, 32)
         silu(2)
         quantize_z([0, 1])
-        interleave("e3", "V", 0, 32)
+        quantize_in("e2")
+        f_unit(4)
         silu(3)
         f_unit(5)
         interleave("e3", "S", 32, 64)
         mult(2, [2, 3])
-        c_unit(5)
+        c_unit_t(5, ORD)
+        interleave("e3", "V", 0, 32)
         mult(3, [2, 3])
-        c_unit(6)
         silu(4)
         quantize_in("e3")
         f_unit(6)
         silu(5)
         f_unit(7)
+        c_unit_t(6, ORD)
         mult(4, [4, 5])
-        c_unit(7)
-        interleave("w2", "S")
+        c_unit_t(7, ORD)
         quantize_z([2, 3])
+        interleave("w2", "S")
         mult(5, [4, 5])
         silu(6)
         quantize_in("w2")

@@ -66,8 +66,8 @@ def tile_picked_schnet_silu_e_kernel(tc, xT, eT, w1, w3, w2, offs, out):
 
         def interleave(name, engine, c0=0, c1=None):
             copy_on[engine](
-                out=grouped[name][:].rearrange("p (c i j) -> p c j i", i=4, j=4)[:, c0:c1],
-                in_=raw[name][:].rearrange("p j (c i) -> p c j i", i=4)[:, c0:c1],
+                out=grouped[name][:].rearrange("p (c i j) -> p c j i", i=2, j=4)[:, 2 * c0 : None if c1 is None else 2 * c1],
+                in_=raw[name][:].rearrange("p j (c i) -> p c j i", i=2)[:, 2 * c0 : None if c1 is None else 2 * c1],
             )
 
         def interleave_w(name, engine, q0, q1):
@@ -238,20 +238,20 @@ def tile_picked_schnet_silu_e_kernel(tc, xT, eT, w1, w3, w2, offs, out):
         f_unit(2)
         f_unit(3)
         c_unit_t(3, ORD)
-        interleave("e2", "S", 32, 64)
+        interleave("e2", "S", 24, 64)
         mult(1, [0, 1])
         c_unit_t(4, ORD)
-        interleave("e2", "V", 0, 32)
+        interleave("e2", "V", 0, 24)
         silu(2)
         quantize_z([0, 1])
         quantize_in("e2")
         f_unit(4)
         silu(3)
         f_unit(5)
-        interleave("e3", "S", 32, 64)
+        interleave("e3", "S", 24, 64)
         mult(2, [2, 3])
         c_unit_t(5, ORD)
-        interleave("e3", "V", 0, 32)
+        interleave("e3", "V", 0, 24)
         mult(3, [2, 3])
         silu(4)
         quantize_in("e3")

@@ -188,6 +188,19 @@ def tile_picked_schnet_silu_e_kernel(tc, xT, eT, w1, w3, w2, offs, out):
             copy_on[engine](out=y[:], in_=oacc[g[0]][:])
             nc.sync.dma_start(out=out[:, g[0] * U : g[0] * U + n], in_=y[:])
 
+        def warm_tensor(passes):
+            idle = psum.tile([P, HALF], F32, name="o_acc", bufs=2)
+            for r in range(passes):
+                nc.tensor.matmul_mx(
+                    out=idle[:],
+                    lhsT=codes["x0"][:, 0:P].bitcast(FP8X4),
+                    lhsT_scale=scales["x0"][:, 0:P],
+                    rhs=codes["x0"][:].bitcast(FP8X4),
+                    rhs_scale=scales["x0"][:],
+                    start=True,
+                    stop=True,
+                )
+
         def warm():
             w = keep.tile([P, 1], F32, name="warm")
             nc.vector.memset(w[:], 0.0)
@@ -212,6 +225,7 @@ def tile_picked_schnet_silu_e_kernel(tc, xT, eT, w1, w3, w2, offs, out):
             gather(t, 1)
         interleave_w("w3", "S", 0, 32)
         quantize_x(0)
+        warm_tensor(3)
         interleave("e0", "V", 0, 32)
         interleave("e0", "S", 32, 64)
         quantize_x(1)

@@ -8,291 +8,201 @@ U32 = mybir.dt.uint32
 U16 = mybir.dt.uint16
 U8 = mybir.dt.uint8
 FP8X4 = mybir.dt.float8_e4m3fn_x4
-SILU = mybir.ActivationFunctionType.Silu
-COPY = mybir.ActivationFunctionType.Copy
-MULT = mybir.AluOpType.mult
 
 P = 128
-T, S, H, N = 4096, 1024, 512, 128
-FLOPS = 2 * 512 * H * S * 2 + 2 * H * N * S
-HALF = 512
-U = 128
+PACK = 4
+K, ATOMS, EDGES, HIDDEN, OUT_ROWS = 512, 4096, 1024, 512, 128
+FLOPS = 2 * (2 * K * HIDDEN * EDGES) + 2 * HIDDEN * OUT_ROWS * EDGES
+
+HALF = EDGES // 2
+UNIT = 128
+CHUNK = 2 * UNIT
+UNITS = EDGES // UNIT
+CHUNKS = EDGES // CHUNK
+C_BANKS, F_BANKS, OUT_BANKS = 3, 2, 3
+VECTOR_EDGES = (128, 128, 96, 96)
+Z_GROUPS = ((0, 1), (2, 3), (4, 5), (6,), (7,))
+W1_TILE_ORDER = (3, 0, 1, 2)
+WARM_PASSES = 3
 
 
 def tile_picked_schnet_silu_e_kernel(tc, xT, eT, w1, w3, w2, offs, out):
     nc = tc.nc
     with ExitStack() as ctx:
         keep = ctx.enter_context(tc.tile_pool(name="keep", bufs=1))
-        psum = ctx.enter_context(tc.psum_pool(name="psum", bufs=3))
+        psum = ctx.enter_context(tc.psum_pool(name="psum", bufs=C_BANKS))
 
-        offsets = keep.tile([P, S // 16], U16, name="offsets")
-        x_rows = xT.rearrange("(p t) n -> p t n", t=4)
-        e_rows = eT.rearrange("(p j) n -> p j n", j=4)
-        planes = [keep.tile([P, T], F32, name=f"plane{t}") for t in range(4)]
-        raw = {}
-        raw["w1"] = keep.tile([P, 4, H], F32, name="w1_raw")
-        raw["w3"] = keep.tile([P, 4, H], F32, name="w3_raw")
-        raw["w2"] = keep.tile([P, 4, N], F32, name="w2_raw")
-        e_cols = {}
-        grouped = {}
-        windows = {}
+        offsets = keep.tile([P, EDGES // 16], U16, name="offsets")
+        planes = [keep.tile([P, ATOMS], F32, name=f"plane{j}") for j in range(PACK)]
+        w1_raw = keep.tile([P, PACK, HIDDEN], F32, name="w1_raw")
+        w3_raw = keep.tile([P, PACK, HIDDEN], F32, name="w3_raw")
+        w2_raw = keep.tile([P, PACK, OUT_ROWS], F32, name="w2_raw")
+        e_raw = [keep.tile([P, PACK, CHUNK], F32, name=f"e_raw{k}") for k in range(CHUNKS)]
+        x_rows = xT.rearrange("(p j) n -> p j n", j=PACK)
+        e_rows = eT.rearrange("(p j) n -> p j n", j=PACK)
 
-        def load_x(t, c0=0, c1=T):
-            nc.sync.dma_start(out=planes[t][:, c0:c1], in_=x_rows[:, t, c0:c1])
+        def load_e(k):
+            nc.sync.dma_start(out=e_raw[k][:], in_=e_rows[:, :, k * CHUNK : (k + 1) * CHUNK])
 
-        def load_w(name, w):
-            nc.sync.dma_start(out=raw[name][:], in_=w.rearrange("(p j) c -> p j c", j=4))
+        nc.sync.dma_start(out=planes[0][:], in_=x_rows[:, 0, :])
+        nc.sync.dma_start(offsets[:], offs)
+        for j in range(1, PACK):
+            nc.sync.dma_start(out=planes[j][:], in_=x_rows[:, j, :])
+        nc.sync.dma_start(out=w3_raw[:], in_=w3.rearrange("(p j) c -> p j c", j=PACK))
+        load_e(0)
+        nc.sync.dma_start(out=w1_raw[:], in_=w1.rearrange("(p j) c -> p j c", j=PACK))
+        for k in range(1, CHUNKS):
+            load_e(k)
+        w2_rows = w2.rearrange("(q t r) c -> r q t c", t=PACK, r=2)
+        for r in range(2):
+            nc.sync.dma_start(out=w2_raw[r:P:2, :, :], in_=w2_rows[r])
 
-        def load_offs():
-            nc.sync.dma_start(offsets[:], offs)
+        table_warm = keep.tile([P, 1], F32, name="table_warm")
+        nc.vector.memset(table_warm[:], 0.0)
+        nc.scalar.activation(out=table_warm[:], in_=table_warm[:], func=mybir.ActivationFunctionType.Silu)
 
-        def load_e(k, c0, c1):
-            e_cols[k] = (c0, c1)
-            raw[f"e{k}"] = keep.tile([P, 4, c1 - c0], F32, name=f"e_raw{k}")
-            grouped[f"e{k}"] = keep.tile([P, (c1 - c0) * 4], BF16, align_bytes=64, name=f"e{k}_grouped")
-            nc.sync.dma_start(out=raw[f"e{k}"][:], in_=e_rows[:, :, c0:c1])
+        x_woven = [keep.tile([P, HALF, PACK], BF16, align_bytes=64, name=f"x_woven{h}") for h in range(2)]
+        e_woven = [keep.tile([P, CHUNK * PACK], BF16, align_bytes=64, name=f"e_woven{k}") for k in range(CHUNKS)]
+        w1_woven = keep.tile([P, HIDDEN * PACK], BF16, align_bytes=64, name="w1_woven")
+        w3_woven = keep.tile([P, HIDDEN * PACK], BF16, align_bytes=64, name="w3_woven")
+        w2_woven = keep.tile([P, OUT_ROWS * PACK], BF16, align_bytes=64, name="w2_woven")
 
-        def load_w2():
-            rows = w2.rearrange("(q t i) c -> i q t c", t=4, i=2)
-            for i in range(2):
-                nc.sync.dma_start(out=raw["w2"][i:P:2, :, :], in_=rows[i])
-
-        copy_on = {"S": nc.scalar.copy, "V": nc.vector.tensor_copy}
-        codes = {}
-        scales = {}
-        for name in ("w1", "w3", "w2"):
-            grouped[name] = keep.tile([P, raw[name].shape[2] * 4], BF16, align_bytes=64, name=f"{name}_grouped")
-        x_grouped = [keep.tile([P, HALF, 4], BF16, align_bytes=64, name=f"x{h}_grouped") for h in range(2)]
-
-        def interleave(name, engine, c0=0, c1=None):
-            copy_on[engine](
-                out=grouped[name][:].rearrange("p (c i j) -> p c j i", i=2, j=4)[:, 2 * c0 : None if c1 is None else 2 * c1],
-                in_=raw[name][:].rearrange("p j (c i) -> p c j i", i=2)[:, 2 * c0 : None if c1 is None else 2 * c1],
+        def weave(copy, woven, raw, columns):
+            pairs = slice(columns.start // 2, columns.stop // 2)
+            copy(
+                out=woven[:].rearrange("p (c r j) -> p c j r", r=2, j=PACK)[:, pairs],
+                in_=raw[:].rearrange("p j (c r) -> p c j r", r=2)[:, pairs],
             )
 
-        def interleave_w(name, engine, q0, q1):
-            copy_on[engine](
-                out=grouped[name][:].rearrange("p (t q i j) -> p q t j i", t=4, i=2, j=4)[:, 2 * q0 : 2 * q1],
-                in_=raw[name][:].rearrange("p j (q t i) -> p q t j i", t=4, i=2)[:, 2 * q0 : 2 * q1],
+        def weave_dealt(copy, woven, raw, tiles, columns):
+            pairs = slice(columns.start // 2, columns.stop // 2)
+            copy(
+                out=woven[:].rearrange("p (t q r j) -> p q t j r", t=PACK, r=2, j=PACK)[:, pairs, tiles],
+                in_=raw[:].rearrange("p j (q t r) -> p q t j r", t=PACK, r=2)[:, pairs, tiles],
             )
 
-        def interleave_t(name, engine, t0, t1, q0=0, q1=32):
-            copy_on[engine](
-                out=grouped[name][:].rearrange("p (t q i j) -> p q t j i", t=4, i=2, j=4)[:, 2 * q0 : 2 * q1, t0:t1],
-                in_=raw[name][:].rearrange("p j (q t i) -> p q t j i", t=4, i=2)[:, 2 * q0 : 2 * q1, t0:t1],
-            )
+        def weave_e(k):
+            weave(nc.vector.tensor_copy, e_woven[k], e_raw[k], slice(0, VECTOR_EDGES[k]))
+            weave(nc.scalar.copy, e_woven[k], e_raw[k], slice(VECTOR_EDGES[k], CHUNK))
 
-        def quantize_t(name, t0, t1):
-            if name not in codes:
-                codes[name] = keep.tile([P, H], U32, align_bytes=64, name=f"{name}_codes")
-                scales[name] = keep.tile([P, H], U8, align_bytes=64, name=f"{name}_scales")
-            nc.vector.quantize_mx(
-                out=codes[name][:, t0 * P : t1 * P].bitcast(FP8X4),
-                scales=scales[name][:, t0 * P : t1 * P],
-                in_=grouped[name][:, t0 * 4 * P : t1 * 4 * P],
-            )
+        def mx_tiles(name, width):
+            codes = keep.tile([P, width], U32, align_bytes=64, name=f"{name}_codes")
+            scales = keep.tile([P, width], U8, align_bytes=64, name=f"{name}_scales")
+            return codes, scales
 
-        def quantize(name, source):
-            width = source.shape[1] // 4
-            codes[name] = keep.tile([P, width], U32, align_bytes=64, name=f"{name}_codes")
-            scales[name] = keep.tile([P, width], U8, align_bytes=64, name=f"{name}_scales")
-            nc.vector.quantize_mx(out=codes[name][:].bitcast(FP8X4), scales=scales[name][:], in_=source)
+        def quantize(operand, columns, woven):
+            codes, scales = operand
+            nc.vector.quantize_mx(out=codes[:, columns].bitcast(FP8X4), scales=scales[:, columns], in_=woven)
 
-        def quantize_in(name):
-            quantize(name, grouped[name][:])
+        def quantize_whole(name, woven):
+            width = woven.shape[1] // PACK
+            operand = mx_tiles(name, width)
+            quantize(operand, slice(0, width), woven)
+            return operand
 
-        def gather(t, h):
-            nc.vector.tensor_copy(
-                x_grouped[h][:, :, t], planes[t][:].indirect(offsets[:, h * HALF // 16 : (h + 1) * HALF // 16])
-            )
-
-        def cast(t, c0, c1, engine):
-            if t not in windows:
-                windows[t] = keep.tile([P, T], BF16, name=f"window{t}")
-            copy_on[engine](out=windows[t][:, c0:c1], in_=planes[t][:, c0:c1])
-
-        def gather_s(t, h):
-            nc.scalar.activation(
-                out=x_grouped[h][:, :, t],
-                in_=windows[t][:].indirect(offsets[:, h * HALF // 16 : (h + 1) * HALF // 16]),
-                func=COPY,
-            )
-
-        def quantize_x(h):
-            quantize(f"x{h}", x_grouped[h][:].rearrange("p n j -> p (n j)"))
-
-        def product(w, x, c0, acc, order=(0, 1, 2, 3)):
-            for t in order:
-                nc.tensor.matmul_mx(
-                    out=acc[:, t, :],
-                    lhsT=codes[w][:, t * P : (t + 1) * P].bitcast(FP8X4),
-                    lhsT_scale=scales[w][:, t * P : (t + 1) * P],
-                    rhs=codes[x][:, c0 : c0 + U].bitcast(FP8X4),
-                    rhs_scale=scales[x][:, c0 : c0 + U],
-                    start=True,
-                    stop=True,
-                )
-
-        filt = {}
-        cacc = {}
-        facc = {}
-        oacc = {}
-        z_tiles = {}
-
-        def f_unit(u):
-            facc[u] = psum.tile([P, 4, U], F32, name="f_acc")
-            k = [k for k in e_cols if e_cols[k][0] <= u * U < e_cols[k][1]][0]
-            product("w3", f"e{k}", u * U - e_cols[k][0], facc[u])
-
-        def silu(u):
-            filt[u] = keep.tile([P, U, 4], F32, name=f"filter{u}")
-            nc.scalar.activation(out=filt[u][:], in_=facc[u][:].rearrange("p t n -> p n t"), func=SILU)
-
-        def c_unit(u):
-            cacc[u] = psum.tile([P, 4, U], F32, name="c_acc")
-            product("w1", f"x{u * U // HALF}", u * U % HALF, cacc[u])
-
-        def c_unit_t(u, order):
-            cacc[u] = psum.tile([P, 4, U], F32, name="c_acc")
-            product("w1", f"x{u * U // HALF}", u * U % HALF, cacc[u], order)
-
-        def mult(u, g):
-            if u == g[0]:
-                z_tiles[g[0]] = keep.tile([P, len(g) * U * 4], BF16, align_bytes=64, name=f"z{g[0]}")
-            col = (u - g[0]) * U
-            nc.vector.tensor_tensor(
-                out=z_tiles[g[0]][:, col * 4 : (col + U) * 4].rearrange("p (n t) -> p n t", t=4),
-                in0=cacc[u][:].rearrange("p t n -> p n t"),
-                in1=filt[u][:],
-                op=MULT,
-            )
-
-        def quantize_z(g):
-            quantize(f"z{g[0]}", z_tiles[g[0]][:])
-
-        def project(g):
-            oacc[g[0]] = psum.tile([P, len(g) * U], F32, name="o_acc", bufs=2)
+        def matmul(acc, stationary, stationary_columns, moving, moving_columns):
             nc.tensor.matmul_mx(
-                out=oacc[g[0]][:],
-                lhsT=codes["w2"][:].bitcast(FP8X4),
-                lhsT_scale=scales["w2"][:],
-                rhs=codes[f"z{g[0]}"][:].bitcast(FP8X4),
-                rhs_scale=scales[f"z{g[0]}"][:],
+                out=acc,
+                lhsT=stationary[0][:, stationary_columns].bitcast(FP8X4),
+                lhsT_scale=stationary[1][:, stationary_columns],
+                rhs=moving[0][:, moving_columns].bitcast(FP8X4),
+                rhs_scale=moving[1][:, moving_columns],
                 start=True,
                 stop=True,
             )
 
-        def store(g, engine):
-            n = len(g) * U
-            y = keep.tile([P, n], F32, name=f"y{g[0]}")
-            copy_on[engine](out=y[:], in_=oacc[g[0]][:])
-            nc.sync.dma_start(out=out[:, g[0] * U : g[0] * U + n], in_=y[:])
+        def product(acc, weight, tile_order, moving, first):
+            for t in tile_order:
+                matmul(acc[:, t, :], weight, slice(t * P, (t + 1) * P), moving, slice(first, first + UNIT))
 
-        def warm_tensor(passes):
-            idle = psum.tile([P, HALF], F32, name="o_acc", bufs=2)
-            for r in range(passes):
-                nc.tensor.matmul_mx(
-                    out=idle[:],
-                    lhsT=codes["x0"][:, 0:P].bitcast(FP8X4),
-                    lhsT_scale=scales["x0"][:, 0:P],
-                    rhs=codes["x0"][:].bitcast(FP8X4),
-                    rhs_scale=scales["x0"][:],
-                    start=True,
-                    stop=True,
-                )
+        x_mx, e_mx, z_mx = {}, {}, {}
+        c_acc, f_acc, filters, z_woven = {}, {}, {}, {}
 
-        def warm():
-            w = keep.tile([P, 1], F32, name="warm")
-            nc.vector.memset(w[:], 0.0)
-            nc.scalar.activation(out=w[:], in_=w[:], func=SILU)
+        def f_products(k):
+            for u in (2 * k, 2 * k + 1):
+                f_acc[u] = psum.tile([P, PACK, UNIT], F32, name="f_acc", bufs=F_BANKS)
+                product(f_acc[u], w3_mx, range(PACK), e_mx[k], u * UNIT % CHUNK)
 
-        ORD = (3, 0, 1, 2)
-        load_x(0)
-        load_offs()
-        load_x(1)
-        load_x(2)
-        load_x(3)
-        load_w("w3", w3)
-        load_e(0,0,256)
-        load_w("w1", w1)
-        load_e(1,256,512)
-        load_e(2,512,768)
-        load_e(3,768,1024)
-        load_w2()
-        warm()
-        for t in range(4):
-            gather(t, 0)
-            gather(t, 1)
-        interleave_w("w3", "S", 0, 32)
-        quantize_x(0)
-        warm_tensor(3)
-        interleave("e0", "V", 0, 32)
-        interleave("e0", "S", 32, 64)
-        quantize_x(1)
-        quantize_in("w3")
-        quantize_in("e0")
-        interleave_t("w1", "S", 3, 4)
-        interleave_t("w1", "V", 0, 2)
-        interleave_t("w1", "V", 2, 3, 0, 16)
-        interleave_t("w1", "S", 2, 3, 16, 32)
-        f_unit(0)
-        f_unit(1)
-        quantize_t("w1", 3, 4)
-        quantize_t("w1", 0, 2)
-        quantize_t("w1", 2, 3)
-        silu(0)
-        c_unit_t(0, ORD)
-        c_unit_t(1, ORD)
-        c_unit_t(2, ORD)
-        interleave("e1", "V", 0, 32)
-        interleave("e1", "S", 32, 64)
-        silu(1)
-        mult(0, [0, 1])
-        quantize_in("e1")
-        f_unit(2)
-        f_unit(3)
-        c_unit_t(3, ORD)
-        interleave("e2", "S", 24, 64)
-        mult(1, [0, 1])
-        c_unit_t(4, ORD)
-        interleave("e2", "V", 0, 24)
-        silu(2)
-        quantize_z([0, 1])
-        quantize_in("e2")
-        f_unit(4)
-        silu(3)
-        f_unit(5)
-        interleave("e3", "S", 24, 64)
-        mult(2, [2, 3])
-        c_unit_t(5, ORD)
-        interleave("e3", "V", 0, 24)
-        mult(3, [2, 3])
-        silu(4)
-        quantize_in("e3")
-        f_unit(6)
-        silu(5)
-        f_unit(7)
-        c_unit_t(6, ORD)
-        mult(4, [4, 5])
-        c_unit_t(7, ORD)
-        quantize_z([2, 3])
-        interleave("w2", "S")
-        mult(5, [4, 5])
-        silu(6)
-        quantize_in("w2")
-        project([0, 1])
-        project([2, 3])
-        silu(7)
-        mult(6, [6])
-        quantize_z([4, 5])
-        store([0, 1], "S")
-        store([2, 3], "S")
-        mult(7, [7])
-        project([4, 5])
-        quantize_z([6])
-        store([4, 5], "S")
-        quantize_z([7])
-        project([6])
-        store([6], "S")
-        project([7])
-        store([7], "V")
+        def c_product(u):
+            c_acc[u] = psum.tile([P, PACK, UNIT], F32, name="c_acc", bufs=C_BANKS)
+            product(c_acc[u], w1_mx, W1_TILE_ORDER, x_mx[u * UNIT // HALF], u * UNIT % HALF)
+
+        def silu(u):
+            filters[u] = keep.tile([P, UNIT, PACK], F32, name=f"filter{u}")
+            nc.scalar.activation(
+                out=filters[u][:], in_=f_acc[u][:].rearrange("p t n -> p n t"), func=mybir.ActivationFunctionType.Silu
+            )
+
+        def multiply(u):
+            group = [g for g in Z_GROUPS if u in g][0]
+            if u == group[0]:
+                z_woven[group] = keep.tile([P, len(group) * UNIT, PACK], BF16, align_bytes=64, name=f"z_woven{u}")
+            first = (u - group[0]) * UNIT
+            nc.vector.tensor_tensor(
+                out=z_woven[group][:, first : first + UNIT, :],
+                in0=c_acc[u][:].rearrange("p t n -> p n t"),
+                in1=filters[u][:],
+                op=mybir.AluOpType.mult,
+            )
+            if u + C_BANKS < UNITS:
+                c_product(u + C_BANKS)
+
+        def quantize_z(group):
+            z_mx[group] = quantize_whole(f"z{group[0]}", z_woven[group][:].rearrange("p n t -> p (n t)"))
+
+        def project_and_store(group, copy):
+            width = len(group) * UNIT
+            acc = psum.tile([P, width], F32, name="out_acc", bufs=OUT_BANKS)
+            matmul(acc[:], w2_mx, slice(0, OUT_ROWS), z_mx[group], slice(0, width))
+            result = keep.tile([P, width], F32, name=f"result{group[0]}")
+            copy(out=result[:], in_=acc[:])
+            nc.sync.dma_start(out=out[:, group[0] * UNIT : group[0] * UNIT + width], in_=result[:])
+
+        for j in range(PACK):
+            for h in range(2):
+                entries = offsets[:, h * HALF // 16 : (h + 1) * HALF // 16]
+                nc.vector.tensor_copy(x_woven[h][:, :, j], planes[j][:].indirect(entries))
+
+        weave_dealt(nc.scalar.copy, w3_woven, w3_raw, slice(0, PACK), slice(0, P))
+        x_mx[0] = quantize_whole("x0", x_woven[0][:].rearrange("p n j -> p (n j)"))
+        tensor_warm = psum.tile([P, HALF], F32, name="out_acc", bufs=OUT_BANKS)
+        for warm_pass in range(WARM_PASSES):
+            matmul(tensor_warm[:], x_mx[0], slice(0, P), x_mx[0], slice(0, HALF))
+        weave_e(0)
+        x_mx[1] = quantize_whole("x1", x_woven[1][:].rearrange("p n j -> p (n j)"))
+        w3_mx = quantize_whole("w3", w3_woven[:])
+        e_mx[0] = quantize_whole("e0", e_woven[0][:])
+
+        weave_dealt(nc.scalar.copy, w1_woven, w1_raw, slice(3, 4), slice(0, P))
+        weave_dealt(nc.vector.tensor_copy, w1_woven, w1_raw, slice(0, 2), slice(0, P))
+        weave_dealt(nc.vector.tensor_copy, w1_woven, w1_raw, slice(2, 3), slice(0, P // 2))
+        weave_dealt(nc.scalar.copy, w1_woven, w1_raw, slice(2, 3), slice(P // 2, P))
+        f_products(0)
+        w1_mx = mx_tiles("w1", HIDDEN)
+        for first, last in ((3, 4), (0, 2), (2, 3)):
+            quantize(w1_mx, slice(first * P, last * P), w1_woven[:, first * P * PACK : last * P * PACK])
+        for u in range(C_BANKS):
+            c_product(u)
+
+        for k in range(CHUNKS):
+            last_turn = k == CHUNKS - 1
+            if last_turn:
+                weave(nc.scalar.copy, w2_woven, w2_raw, slice(0, OUT_ROWS))
+            else:
+                weave_e(k + 1)
+            silu(2 * k)
+            silu(2 * k + 1)
+            multiply(2 * k)
+            if last_turn:
+                w2_mx = quantize_whole("w2", w2_woven[:])
+            else:
+                e_mx[k + 1] = quantize_whole(f"e{k + 1}", e_woven[k + 1][:])
+                f_products(k + 1)
+            multiply(2 * k + 1)
+            for group in Z_GROUPS:
+                if group[0] // 2 == k:
+                    quantize_z(group)
+
+        for group in Z_GROUPS[:-1]:
+            project_and_store(group, nc.scalar.copy)
+        project_and_store(Z_GROUPS[-1], nc.vector.tensor_copy)

@@ -24,6 +24,7 @@ VECTOR_EDGES = (128, 128, 96, 96)
 Z_GROUPS = ((0, 1), (2, 3), (4, 5), (6,), (7,))
 W1_TILE_ORDER = (3, 0, 1, 2)
 WARM_PASSES = 3
+STORE_ENDS = (2, 6, 7, 8)
 
 
 def tile_picked_schnet_silu_e_kernel(tc, xT, eT, w1, w3, w2, offs, out):
@@ -33,7 +34,8 @@ def tile_picked_schnet_silu_e_kernel(tc, xT, eT, w1, w3, w2, offs, out):
         psum = ctx.enter_context(tc.psum_pool(name="psum", bufs=C_BANKS))
 
         offsets = keep.tile([P, EDGES // 16], U16, name="offsets")
-        planes = [keep.tile([P, ATOMS], F32, name=f"plane{j}") for j in range(PACK)]
+        first_planes = keep.tile([P, 2, ATOMS], F32, name="first_planes")
+        planes = {j: keep.tile([P, ATOMS], F32, name=f"plane{j}") for j in range(2, PACK)}
         w1_raw = keep.tile([P, PACK, HIDDEN], F32, name="w1_raw")
         w3_raw = keep.tile([P, PACK, HIDDEN], F32, name="w3_raw")
         w2_raw = keep.tile([P, PACK, OUT_ROWS], F32, name="w2_raw")
@@ -44,9 +46,9 @@ def tile_picked_schnet_silu_e_kernel(tc, xT, eT, w1, w3, w2, offs, out):
         def load_e(k):
             nc.sync.dma_start(out=e_raw[k][:], in_=e_rows[:, :, k * CHUNK : (k + 1) * CHUNK])
 
-        nc.sync.dma_start(out=planes[0][:], in_=x_rows[:, 0, :])
+        nc.sync.dma_start(out=first_planes[:], in_=x_rows[:, 0:2, :])
         nc.sync.dma_start(offsets[:], offs)
-        for j in range(1, PACK):
+        for j in range(2, PACK):
             nc.sync.dma_start(out=planes[j][:], in_=x_rows[:, j, :])
         nc.sync.dma_start(out=w3_raw[:], in_=w3.rearrange("(p j) c -> p j c", j=PACK))
         load_e(0)
@@ -150,15 +152,26 @@ def tile_picked_schnet_silu_e_kernel(tc, xT, eT, w1, w3, w2, offs, out):
         def quantize_z(group):
             z_mx[group] = quantize_whole(f"z{group[0]}", z_woven[group][:].rearrange("p n t -> p (n t)"))
 
+        result = keep.tile([P, EDGES], F32, name="result")
+
         def project_and_store(group, copy):
             width = len(group) * UNIT
             acc = psum.tile([P, width], F32, name="out_acc", bufs=OUT_BANKS)
             matmul(acc[:], w2_mx, slice(0, OUT_ROWS), z_mx[group], slice(0, width))
-            result = keep.tile([P, width], F32, name=f"result{group[0]}")
-            copy(out=result[:], in_=acc[:])
-            nc.sync.dma_start(out=out[:, group[0] * UNIT : group[0] * UNIT + width], in_=result[:])
+            copy(out=result[:, group[0] * UNIT : group[0] * UNIT + width], in_=acc[:])
+            if group[-1] + 1 in STORE_ENDS:
+                first = ([0] + list(STORE_ENDS))[STORE_ENDS.index(group[-1] + 1)] * UNIT
+                last = (group[-1] + 1) * UNIT
+                nc.sync.dma_start(out=out[:, first:last], in_=result[:, first:last])
 
-        for j in range(PACK):
+        picked = keep.tile([P, 2, EDGES], F32, name="picked")
+        for j in range(2):
+            nc.vector.tensor_copy(picked[:, j, :], first_planes[:, j, :].indirect(offsets[:]))
+        for h in range(2):
+            nc.scalar.copy(
+                out=x_woven[h][:, :, 0:2], in_=picked[:, :, h * HALF : (h + 1) * HALF].rearrange("p j n -> p n j")
+            )
+        for j in range(2, PACK):
             for h in range(2):
                 entries = offsets[:, h * HALF // 16 : (h + 1) * HALF // 16]
                 nc.vector.tensor_copy(x_woven[h][:, :, j], planes[j][:].indirect(entries))

@@ -39,7 +39,7 @@ def tile_picked_schnet_silu_e_kernel(tc, xT, eT, w1, w3, w2, offs, out):
         w1_raw = keep.tile([P, PACK, HIDDEN], F32, name="w1_raw")
         w3_raw = keep.tile([P, PACK, HIDDEN], F32, name="w3_raw")
         w2_raw = keep.tile([P, PACK, OUT_ROWS], F32, name="w2_raw")
-        e_raw = [keep.tile([P, PACK, CHUNK], F32, name=f"e_raw{k}") for k in range(CHUNKS)]
+        e_raw = [keep.tile([P, PACK, CHUNK], F32, align_bytes=64, name=f"e_raw{k}") for k in range(CHUNKS)]
         x_rows = xT.rearrange("(p j) n -> p j n", j=PACK)
         e_rows = eT.rearrange("(p j) n -> p j n", j=PACK)
 
@@ -87,8 +87,8 @@ def tile_picked_schnet_silu_e_kernel(tc, xT, eT, w1, w3, w2, offs, out):
             weave(nc.vector.tensor_copy, e_woven[k], e_raw[k], slice(0, VECTOR_EDGES[k]))
             weave(nc.scalar.copy, e_woven[k], e_raw[k], slice(VECTOR_EDGES[k], CHUNK))
 
-        def mx_tiles(name, width):
-            codes = keep.tile([P, width], U32, align_bytes=64, name=f"{name}_codes")
+        def mx_tiles(name, width, tag=""):
+            codes = keep.tile([P, width], U32, align_bytes=64, name=f"{name}_codes", tag=tag)
             scales = keep.tile([P, width], U8, align_bytes=64, name=f"{name}_scales")
             return codes, scales
 
@@ -96,9 +96,9 @@ def tile_picked_schnet_silu_e_kernel(tc, xT, eT, w1, w3, w2, offs, out):
             codes, scales = operand
             nc.vector.quantize_mx(out=codes[:, columns].bitcast(FP8X4), scales=scales[:, columns], in_=woven)
 
-        def quantize_whole(name, woven):
+        def quantize_whole(name, woven, tag=""):
             width = woven.shape[1] // PACK
-            operand = mx_tiles(name, width)
+            operand = mx_tiles(name, width, tag)
             quantize(operand, slice(0, width), woven)
             return operand
 
@@ -138,7 +138,9 @@ def tile_picked_schnet_silu_e_kernel(tc, xT, eT, w1, w3, w2, offs, out):
         def multiply(u):
             group = [g for g in Z_GROUPS if u in g][0]
             if u == group[0]:
-                z_woven[group] = keep.tile([P, len(group) * UNIT, PACK], BF16, align_bytes=64, name=f"z_woven{u}")
+                z_woven[group] = keep.tile(
+                    [P, len(group) * UNIT, PACK], BF16, align_bytes=64, name=f"z_woven{u}", tag="e_raw1" if u == 0 else ""
+                )
             first = (u - group[0]) * UNIT
             nc.vector.tensor_tensor(
                 out=z_woven[group][:, first : first + UNIT, :],
@@ -150,7 +152,7 @@ def tile_picked_schnet_silu_e_kernel(tc, xT, eT, w1, w3, w2, offs, out):
                 c_product(u + C_BANKS)
 
         def quantize_z(group):
-            z_mx[group] = quantize_whole(f"z{group[0]}", z_woven[group][:].rearrange("p n t -> p (n t)"))
+            z_mx[group] = quantize_whole(f"z{group[0]}", z_woven[group][:].rearrange("p n t -> p (n t)"), {0: "e_raw2", 2: "e_raw3"}.get(group[0], ""))
 
         result = keep.tile([P, EDGES], F32, name="result")
 
@@ -176,6 +178,22 @@ def tile_picked_schnet_silu_e_kernel(tc, xT, eT, w1, w3, w2, offs, out):
                 entries = offsets[:, h * HALF // 16 : (h + 1) * HALF // 16]
                 nc.vector.tensor_copy(x_woven[h][:, :, j], planes[j][:].indirect(entries))
 
+        V, S = nc.vector.tensor_copy, nc.scalar.copy
+        starts = [0, 1024 - 4 * 64]
+        starts.append(starts[1] + 1024 - 4 * 96)
+        starts.append(starts[2] + 1024 - 4 * 0)
+        stage = keep.tile([P, starts[3] + 512], BF16, align_bytes=64, name="stage")
+        for k in range(1, 4):
+            e_woven[k] = stage[:, starts[k - 1] : starts[k - 1] + 1024]
+        w2_woven = stage[:, starts[3] : starts[3] + 512]
+        def G(woven, raw, n):
+            nc.gpsimd.tensor_scalar(
+                out=woven.rearrange("p (c j) -> p c j", j=PACK)[:, 0:n],
+                in0=raw[:].rearrange("p j c -> p c j")[:, 0:n],
+                scalar1=1.0, scalar2=0.0, op0=mybir.AluOpType.mult, op1=mybir.AluOpType.add,
+            )
+        def qe(k):
+            e_mx[k] = quantize_whole(f"e{k}", e_woven[k][:])
         weave_dealt(nc.scalar.copy, w3_woven, w3_raw, slice(0, PACK), slice(0, P))
         x_mx[0] = quantize_whole("x0", x_woven[0][:].rearrange("p n j -> p (n j)"))
         tensor_warm = psum.tile([P, HALF], F32, name="out_acc", bufs=OUT_BANKS)
@@ -185,7 +203,6 @@ def tile_picked_schnet_silu_e_kernel(tc, xT, eT, w1, w3, w2, offs, out):
         x_mx[1] = quantize_whole("x1", x_woven[1][:].rearrange("p n j -> p (n j)"))
         w3_mx = quantize_whole("w3", w3_woven[:])
         e_mx[0] = quantize_whole("e0", e_woven[0][:])
-
         weave_dealt(nc.scalar.copy, w1_woven, w1_raw, slice(3, 4), slice(0, P))
         weave_dealt(nc.vector.tensor_copy, w1_woven, w1_raw, slice(0, 2), slice(0, P))
         weave_dealt(nc.vector.tensor_copy, w1_woven, w1_raw, slice(2, 3), slice(0, P // 2))
@@ -196,26 +213,44 @@ def tile_picked_schnet_silu_e_kernel(tc, xT, eT, w1, w3, w2, offs, out):
             quantize(w1_mx, slice(first * P, last * P), w1_woven[:, first * P * PACK : last * P * PACK])
         for u in range(C_BANKS):
             c_product(u)
+        silu(0)
+        weave(V, e_woven[1], e_raw[1], slice(0, 208))
+        weave(S, e_woven[1], e_raw[1], slice(208, 256))
+        silu(1)
+        qe(1)
+        f_products(1)
+        G(e_woven[2], e_raw[2], 64)
 
-        for k in range(CHUNKS):
-            last_turn = k == CHUNKS - 1
-            if last_turn:
-                weave(nc.scalar.copy, w2_woven, w2_raw, slice(0, OUT_ROWS))
-            else:
-                weave_e(k + 1)
-            silu(2 * k)
-            silu(2 * k + 1)
-            multiply(2 * k)
-            if last_turn:
-                w2_mx = quantize_whole("w2", w2_woven[:])
-            else:
-                e_mx[k + 1] = quantize_whole(f"e{k + 1}", e_woven[k + 1][:])
-                f_products(k + 1)
-            multiply(2 * k + 1)
-            for group in Z_GROUPS:
-                if group[0] // 2 == k:
-                    quantize_z(group)
+        weave(S, e_woven[2], e_raw[2], slice(64, 256))
+        multiply(0)
+        multiply(1)
+        silu(2)
+        silu(3)
+        qe(2)
+        f_products(2)
+        quantize_z((0, 1))
+        G(e_woven[3], e_raw[3], 96)
 
+        weave(S, e_woven[3], e_raw[3], slice(96, 256))
+        multiply(2)
+        multiply(3)
+        silu(4)
+        silu(5)
+        qe(3)
+        f_products(3)
+        quantize_z((2, 3))
+
+        weave(S, w2_woven, w2_raw, slice(0, 128))
+        multiply(4)
+        multiply(5)
+        silu(6)
+        silu(7)
+        w2_mx = quantize_whole("w2", w2_woven[:])
+        quantize_z((4, 5))
+        multiply(6)
+        multiply(7)
+        quantize_z((6,))
+        quantize_z((7,))
         for group in Z_GROUPS[:-1]:
             project_and_store(group, nc.scalar.copy)
         project_and_store(Z_GROUPS[-1], nc.vector.tensor_copy)

@@ -20,7 +20,8 @@ CHUNK = 2 * UNIT
 UNITS = EDGES // UNIT
 CHUNKS = EDGES // CHUNK
 C_BANKS, F_BANKS, OUT_BANKS = 3, 2, 3
-VECTOR_EDGES = (128, 128, 96, 96)
+VECTOR_EDGES = (128, 208)
+GPSIMD_COLUMNS = (64, 104, 88)
 Z_GROUPS = ((0, 1), (2, 3), (4, 5), (6,), (7,))
 W1_TILE_ORDER = (3, 0, 1, 2)
 WARM_PASSES = 3
@@ -64,15 +65,20 @@ def tile_picked_schnet_silu_e_kernel(tc, xT, eT, w1, w3, w2, offs, out):
         nc.scalar.activation(out=table_warm[:], in_=table_warm[:], func=mybir.ActivationFunctionType.Silu)
 
         x_woven = [keep.tile([P, HALF, PACK], BF16, align_bytes=64, name=f"x_woven{h}") for h in range(2)]
-        e_woven = [keep.tile([P, CHUNK * PACK], BF16, align_bytes=64, name=f"e_woven{k}") for k in range(CHUNKS)]
+        e0_woven = keep.tile([P, CHUNK * PACK], BF16, align_bytes=64, name="e0_woven")
         w1_woven = keep.tile([P, HIDDEN * PACK], BF16, align_bytes=64, name="w1_woven")
         w3_woven = keep.tile([P, HIDDEN * PACK], BF16, align_bytes=64, name="w3_woven")
-        w2_woven = keep.tile([P, OUT_ROWS * PACK], BF16, align_bytes=64, name="w2_woven")
+        late_starts = [0]
+        for columns in GPSIMD_COLUMNS:
+            late_starts.append(late_starts[-1] + (CHUNK - columns) * PACK)
+        late = keep.tile([P, late_starts[-1] + OUT_ROWS * PACK], BF16, align_bytes=64, name="late")
+        e_woven = [e0_woven[:]] + [late[:, first : first + CHUNK * PACK] for first in late_starts[:-1]]
+        w2_woven = late[:, late_starts[-1] : late_starts[-1] + OUT_ROWS * PACK]
 
         def weave(copy, woven, raw, columns):
             pairs = slice(columns.start // 2, columns.stop // 2)
             copy(
-                out=woven[:].rearrange("p (c r j) -> p c j r", r=2, j=PACK)[:, pairs],
+                out=woven.rearrange("p (c r j) -> p c j r", r=2, j=PACK)[:, pairs],
                 in_=raw[:].rearrange("p j (c r) -> p c j r", r=2)[:, pairs],
             )
 
@@ -83,12 +89,19 @@ def tile_picked_schnet_silu_e_kernel(tc, xT, eT, w1, w3, w2, offs, out):
                 in_=raw[:].rearrange("p j (q t r) -> p q t j r", t=PACK, r=2)[:, pairs, tiles],
             )
 
-        def weave_e(k):
-            weave(nc.vector.tensor_copy, e_woven[k], e_raw[k], slice(0, VECTOR_EDGES[k]))
-            weave(nc.scalar.copy, e_woven[k], e_raw[k], slice(VECTOR_EDGES[k], CHUNK))
+        def weave_late(woven, raw, gpsimd_columns):
+            nc.gpsimd.tensor_scalar(
+                out=woven.rearrange("p (c j) -> p c j", j=PACK)[:, 0:gpsimd_columns],
+                in0=raw[:].rearrange("p j c -> p c j")[:, 0:gpsimd_columns],
+                scalar1=1.0,
+                scalar2=0.0,
+                op0=mybir.AluOpType.mult,
+                op1=mybir.AluOpType.add,
+            )
+            weave(nc.scalar.copy, woven, raw, slice(gpsimd_columns, raw.shape[2]))
 
-        def mx_tiles(name, width, tag=""):
-            codes = keep.tile([P, width], U32, align_bytes=64, name=f"{name}_codes", tag=tag)
+        def mx_tiles(name, width, codes_tag=""):
+            codes = keep.tile([P, width], U32, align_bytes=64, name=f"{name}_codes", tag=codes_tag)
             scales = keep.tile([P, width], U8, align_bytes=64, name=f"{name}_scales")
             return codes, scales
 
@@ -96,9 +109,9 @@ def tile_picked_schnet_silu_e_kernel(tc, xT, eT, w1, w3, w2, offs, out):
             codes, scales = operand
             nc.vector.quantize_mx(out=codes[:, columns].bitcast(FP8X4), scales=scales[:, columns], in_=woven)
 
-        def quantize_whole(name, woven, tag=""):
+        def quantize_whole(name, woven, codes_tag=""):
             width = woven.shape[1] // PACK
-            operand = mx_tiles(name, width, tag)
+            operand = mx_tiles(name, width, codes_tag)
             quantize(operand, slice(0, width), woven)
             return operand
 
@@ -135,12 +148,16 @@ def tile_picked_schnet_silu_e_kernel(tc, xT, eT, w1, w3, w2, offs, out):
                 out=filters[u][:], in_=f_acc[u][:].rearrange("p t n -> p n t"), func=mybir.ActivationFunctionType.Silu
             )
 
+        def z_tile(group):
+            if group == Z_GROUPS[-2]:
+                return w2_woven.rearrange("p (n t) -> p n t", t=PACK)
+            tag = "e_raw1" if group == Z_GROUPS[0] else ""
+            return keep.tile([P, len(group) * UNIT, PACK], BF16, align_bytes=64, name=f"z_woven{group[0]}", tag=tag)
+
         def multiply(u):
             group = [g for g in Z_GROUPS if u in g][0]
             if u == group[0]:
-                z_woven[group] = keep.tile(
-                    [P, len(group) * UNIT, PACK], BF16, align_bytes=64, name=f"z_woven{u}", tag="e_raw1" if u == 0 else ""
-                )
+                z_woven[group] = z_tile(group)
             first = (u - group[0]) * UNIT
             nc.vector.tensor_tensor(
                 out=z_woven[group][:, first : first + UNIT, :],
@@ -151,8 +168,8 @@ def tile_picked_schnet_silu_e_kernel(tc, xT, eT, w1, w3, w2, offs, out):
             if u + C_BANKS < UNITS:
                 c_product(u + C_BANKS)
 
-        def quantize_z(group):
-            z_mx[group] = quantize_whole(f"z{group[0]}", z_woven[group][:].rearrange("p n t -> p (n t)"), {0: "e_raw2", 2: "e_raw3"}.get(group[0], ""))
+        def quantize_z(group, codes_tag=""):
+            z_mx[group] = quantize_whole(f"z{group[0]}", z_woven[group][:].rearrange("p n t -> p (n t)"), codes_tag)
 
         result = keep.tile([P, EDGES], F32, name="result")
 
@@ -178,31 +195,17 @@ def tile_picked_schnet_silu_e_kernel(tc, xT, eT, w1, w3, w2, offs, out):
                 entries = offsets[:, h * HALF // 16 : (h + 1) * HALF // 16]
                 nc.vector.tensor_copy(x_woven[h][:, :, j], planes[j][:].indirect(entries))
 
-        V, S = nc.vector.tensor_copy, nc.scalar.copy
-        starts = [0, 1024 - 4 * 64]
-        starts.append(starts[1] + 1024 - 4 * 96)
-        starts.append(starts[2] + 1024 - 4 * 0)
-        stage = keep.tile([P, starts[3] + 512], BF16, align_bytes=64, name="stage")
-        for k in range(1, 4):
-            e_woven[k] = stage[:, starts[k - 1] : starts[k - 1] + 1024]
-        w2_woven = stage[:, starts[3] : starts[3] + 512]
-        def G(woven, raw, n):
-            nc.gpsimd.tensor_scalar(
-                out=woven.rearrange("p (c j) -> p c j", j=PACK)[:, 0:n],
-                in0=raw[:].rearrange("p j c -> p c j")[:, 0:n],
-                scalar1=1.0, scalar2=0.0, op0=mybir.AluOpType.mult, op1=mybir.AluOpType.add,
-            )
-        def qe(k):
-            e_mx[k] = quantize_whole(f"e{k}", e_woven[k][:])
         weave_dealt(nc.scalar.copy, w3_woven, w3_raw, slice(0, PACK), slice(0, P))
         x_mx[0] = quantize_whole("x0", x_woven[0][:].rearrange("p n j -> p (n j)"))
         tensor_warm = psum.tile([P, HALF], F32, name="out_acc", bufs=OUT_BANKS)
         for warm_pass in range(WARM_PASSES):
             matmul(tensor_warm[:], x_mx[0], slice(0, P), x_mx[0], slice(0, HALF))
-        weave_e(0)
+        weave(nc.vector.tensor_copy, e_woven[0], e_raw[0], slice(0, VECTOR_EDGES[0]))
+        weave(nc.scalar.copy, e_woven[0], e_raw[0], slice(VECTOR_EDGES[0], CHUNK))
         x_mx[1] = quantize_whole("x1", x_woven[1][:].rearrange("p n j -> p (n j)"))
         w3_mx = quantize_whole("w3", w3_woven[:])
-        e_mx[0] = quantize_whole("e0", e_woven[0][:])
+        e_mx[0] = quantize_whole("e0", e_woven[0])
+
         weave_dealt(nc.scalar.copy, w1_woven, w1_raw, slice(3, 4), slice(0, P))
         weave_dealt(nc.vector.tensor_copy, w1_woven, w1_raw, slice(0, 2), slice(0, P))
         weave_dealt(nc.vector.tensor_copy, w1_woven, w1_raw, slice(2, 3), slice(0, P // 2))
@@ -214,43 +217,34 @@ def tile_picked_schnet_silu_e_kernel(tc, xT, eT, w1, w3, w2, offs, out):
         for u in range(C_BANKS):
             c_product(u)
         silu(0)
-        weave(V, e_woven[1], e_raw[1], slice(0, 208))
-        weave(S, e_woven[1], e_raw[1], slice(208, 256))
+        weave(nc.vector.tensor_copy, e_woven[1], e_raw[1], slice(0, VECTOR_EDGES[1]))
+        weave(nc.scalar.copy, e_woven[1], e_raw[1], slice(VECTOR_EDGES[1], CHUNK))
         silu(1)
-        qe(1)
+        e_mx[1] = quantize_whole("e1", e_woven[1])
         f_products(1)
-        G(e_woven[2], e_raw[2], 64)
 
-        weave(S, e_woven[2], e_raw[2], slice(64, 256))
-        multiply(0)
-        multiply(1)
-        silu(2)
-        silu(3)
-        qe(2)
-        f_products(2)
-        quantize_z((0, 1))
-        G(e_woven[3], e_raw[3], 96)
+        for k in range(CHUNKS - 1):
+            ahead = k + 2
+            if ahead < CHUNKS:
+                weave_late(e_woven[ahead], e_raw[ahead], GPSIMD_COLUMNS[k])
+            else:
+                weave_late(w2_woven, w2_raw, GPSIMD_COLUMNS[k])
+            multiply(2 * k)
+            multiply(2 * k + 1)
+            silu(2 * k + 2)
+            silu(2 * k + 3)
+            if ahead < CHUNKS:
+                e_mx[ahead] = quantize_whole(f"e{ahead}", e_woven[ahead])
+                f_products(ahead)
+                quantize_z(Z_GROUPS[k], f"e_raw{ahead}")
+            else:
+                w2_mx = quantize_whole("w2", w2_woven)
+                quantize_z(Z_GROUPS[k])
+        for group in Z_GROUPS[-2:]:
+            multiply(group[0])
+        for group in Z_GROUPS[-2:]:
+            quantize_z(group)
 
-        weave(S, e_woven[3], e_raw[3], slice(96, 256))
-        multiply(2)
-        multiply(3)
-        silu(4)
-        silu(5)
-        qe(3)
-        f_products(3)
-        quantize_z((2, 3))
-
-        weave(S, w2_woven, w2_raw, slice(0, 128))
-        multiply(4)
-        multiply(5)
-        silu(6)
-        silu(7)
-        w2_mx = quantize_whole("w2", w2_woven[:])
-        quantize_z((4, 5))
-        multiply(6)
-        multiply(7)
-        quantize_z((6,))
-        quantize_z((7,))
         for group in Z_GROUPS[:-1]:
             project_and_store(group, nc.scalar.copy)
         project_and_store(Z_GROUPS[-1], nc.vector.tensor_copy)

@@ -8,6 +8,7 @@ U32 = mybir.dt.uint32
 U16 = mybir.dt.uint16
 U8 = mybir.dt.uint8
 FP8X4 = mybir.dt.float8_e4m3fn_x4
+ACT = mybir.ActivationFunctionType
 
 P = 128
 PACK = 4
@@ -16,15 +17,11 @@ FLOPS = 2 * (2 * K * HIDDEN * EDGES) + 2 * HIDDEN * OUT_ROWS * EDGES
 
 HALF = EDGES // 2
 UNIT = 128
-CHUNK = 2 * UNIT
 UNITS = EDGES // UNIT
-CHUNKS = EDGES // CHUNK
+PIECES = (2, 2, 2, 2)
 C_BANKS, F_BANKS, OUT_BANKS = 3, 2, 3
-VECTOR_EDGES = (128, 208)
 GPSIMD_COLUMNS = (64, 104, 88)
 Z_GROUPS = ((0, 1), (2, 3), (4, 5), (6,), (7,))
-W1_TILE_ORDER = (3, 0, 1, 2)
-WARM_PASSES = 3
 STORE_ENDS = (2, 6, 7, 8)
 
 
@@ -37,42 +34,42 @@ def tile_picked_schnet_silu_e_kernel(tc, xT, eT, w1, w3, w2, offs, out):
         offsets = keep.tile([P, EDGES // 16], U16, name="offsets")
         first_planes = keep.tile([P, 2, ATOMS], F32, name="first_planes")
         planes = {j: keep.tile([P, ATOMS], F32, name=f"plane{j}") for j in range(2, PACK)}
-        w1_raw = keep.tile([P, PACK, HIDDEN], F32, name="w1_raw")
-        w3_raw = keep.tile([P, PACK, HIDDEN], F32, name="w3_raw")
+        w1_raw = [keep.tile([P, PACK, HIDDEN // 2], F32, align_bytes=64, name=f"w1_raw{h}") for h in range(2)]
+        w3_raw = keep.tile([P, PACK, HIDDEN], F32, align_bytes=64, name="w3_raw")
         w2_raw = keep.tile([P, PACK, OUT_ROWS], F32, name="w2_raw")
-        e_raw = [keep.tile([P, PACK, CHUNK], F32, align_bytes=64, name=f"e_raw{k}") for k in range(CHUNKS)]
+        e_raw = [keep.tile([P, PACK, n * UNIT], F32, align_bytes=64, name=f"e_raw{k}") for k, n in enumerate(PIECES)]
+        e_first = [sum(PIECES[:k]) for k in range(len(PIECES))]
         x_rows = xT.rearrange("(p j) n -> p j n", j=PACK)
         e_rows = eT.rearrange("(p j) n -> p j n", j=PACK)
-
-        def load_e(k):
-            nc.sync.dma_start(out=e_raw[k][:], in_=e_rows[:, :, k * CHUNK : (k + 1) * CHUNK])
 
         nc.sync.dma_start(out=first_planes[:], in_=x_rows[:, 0:2, :])
         nc.sync.dma_start(offsets[:], offs)
         for j in range(2, PACK):
             nc.sync.dma_start(out=planes[j][:], in_=x_rows[:, j, :])
         nc.sync.dma_start(out=w3_raw[:], in_=w3.rearrange("(p j) c -> p j c", j=PACK))
-        load_e(0)
-        nc.sync.dma_start(out=w1_raw[:], in_=w1.rearrange("(p j) c -> p j c", j=PACK))
-        for k in range(1, CHUNKS):
-            load_e(k)
+        w1_rows = w1.rearrange("(p j) c -> p j c", j=PACK)
+        for k, n in enumerate(PIECES):
+            nc.sync.dma_start(out=e_raw[k][:], in_=e_rows[:, :, e_first[k] * UNIT : (e_first[k] + n) * UNIT])
+            if k == 0:
+                for h in range(2):
+                    nc.sync.dma_start(out=w1_raw[h][:], in_=w1_rows[:, :, h * HIDDEN // 2 : (h + 1) * HIDDEN // 2])
         w2_rows = w2.rearrange("(q t r) c -> r q t c", t=PACK, r=2)
         for r in range(2):
             nc.sync.dma_start(out=w2_raw[r:P:2, :, :], in_=w2_rows[r])
 
         table_warm = keep.tile([P, 1], F32, name="table_warm")
         nc.vector.memset(table_warm[:], 0.0)
-        nc.scalar.activation(out=table_warm[:], in_=table_warm[:], func=mybir.ActivationFunctionType.Silu)
+        nc.scalar.activation(out=table_warm[:], in_=table_warm[:], func=ACT.Silu)
 
         x_woven = [keep.tile([P, HALF, PACK], BF16, align_bytes=64, name=f"x_woven{h}") for h in range(2)]
-        e0_woven = keep.tile([P, CHUNK * PACK], BF16, align_bytes=64, name="e0_woven")
         w1_woven = keep.tile([P, HIDDEN * PACK], BF16, align_bytes=64, name="w1_woven")
         w3_woven = keep.tile([P, HIDDEN * PACK], BF16, align_bytes=64, name="w3_woven")
+        early = [keep.tile([P, 2 * UNIT * PACK], BF16, align_bytes=64, name="e_woven0")]
         late_starts = [0]
         for columns in GPSIMD_COLUMNS:
-            late_starts.append(late_starts[-1] + (CHUNK - columns) * PACK)
+            late_starts.append(late_starts[-1] + (2 * UNIT - columns) * PACK)
         late = keep.tile([P, late_starts[-1] + OUT_ROWS * PACK], BF16, align_bytes=64, name="late")
-        e_woven = [e0_woven[:]] + [late[:, first : first + CHUNK * PACK] for first in late_starts[:-1]]
+        e_woven = [t[:] for t in early] + [late[:, first : first + 2 * UNIT * PACK] for first in late_starts[:-1]]
         w2_woven = late[:, late_starts[-1] : late_starts[-1] + OUT_ROWS * PACK]
 
         def weave(copy, woven, raw, columns):
@@ -82,23 +79,29 @@ def tile_picked_schnet_silu_e_kernel(tc, xT, eT, w1, w3, w2, offs, out):
                 in_=raw[:].rearrange("p j (c r) -> p c j r", r=2)[:, pairs],
             )
 
-        def weave_dealt(copy, woven, raw, tiles, columns):
+        def weave_dealt(copy, woven, raw, tiles, columns, first=0):
             pairs = slice(columns.start // 2, columns.stop // 2)
+            places = slice((first + columns.start) // 2, (first + columns.stop) // 2)
             copy(
-                out=woven[:].rearrange("p (t q r j) -> p q t j r", t=PACK, r=2, j=PACK)[:, pairs, tiles],
+                out=woven[:].rearrange("p (t q r j) -> p q t j r", t=PACK, r=2, j=PACK)[:, places, tiles],
                 in_=raw[:].rearrange("p j (q t r) -> p q t j r", t=PACK, r=2)[:, pairs, tiles],
             )
 
-        def weave_late(woven, raw, gpsimd_columns):
-            nc.gpsimd.tensor_scalar(
-                out=woven.rearrange("p (c j) -> p c j", j=PACK)[:, 0:gpsimd_columns],
-                in0=raw[:].rearrange("p j c -> p c j")[:, 0:gpsimd_columns],
-                scalar1=1.0,
-                scalar2=0.0,
-                op0=mybir.AluOpType.mult,
-                op1=mybir.AluOpType.add,
-            )
-            weave(nc.scalar.copy, woven, raw, slice(gpsimd_columns, raw.shape[2]))
+        def weave_shared(woven, raw, gpsimd_columns, vector_columns):
+            width = raw.shape[2]
+            if gpsimd_columns:
+                nc.gpsimd.tensor_scalar(
+                    out=woven.rearrange("p (c j) -> p c j", j=PACK)[:, 0:gpsimd_columns],
+                    in0=raw[:].rearrange("p j c -> p c j")[:, 0:gpsimd_columns],
+                    scalar1=1.0,
+                    scalar2=0.0,
+                    op0=mybir.AluOpType.mult,
+                    op1=mybir.AluOpType.add,
+                )
+            if gpsimd_columns + vector_columns < width:
+                weave(nc.scalar.copy, woven, raw, slice(gpsimd_columns, width - vector_columns))
+            if vector_columns:
+                weave(nc.vector.tensor_copy, woven, raw, slice(width - vector_columns, width))
 
         def mx_tiles(name, width, codes_tag=""):
             codes = keep.tile([P, width], U32, align_bytes=64, name=f"{name}_codes", tag=codes_tag)
@@ -126,33 +129,36 @@ def tile_picked_schnet_silu_e_kernel(tc, xT, eT, w1, w3, w2, offs, out):
                 stop=True,
             )
 
-        def product(acc, weight, tile_order, moving, first):
-            for t in tile_order:
+        def product(acc, weight, moving, first):
+            for t in (2, 3, 0, 1):
                 matmul(acc[:, t, :], weight, slice(t * P, (t + 1) * P), moving, slice(first, first + UNIT))
 
-        x_mx, e_mx, z_mx = {}, {}, {}
+        x_mx, z_mx = {}, {}
         c_acc, f_acc, filters, z_woven = {}, {}, {}, {}
 
-        def f_products(k):
-            for u in (2 * k, 2 * k + 1):
+        def quantize_e(k):
+            e_mx = quantize_whole(f"e{k}", e_woven[k])
+            for n in range(PIECES[k]):
+                u = e_first[k] + n
                 f_acc[u] = psum.tile([P, PACK, UNIT], F32, name="f_acc", bufs=F_BANKS)
-                product(f_acc[u], w3_mx, range(PACK), e_mx[k], u * UNIT % CHUNK)
+                product(f_acc[u], w3_mx, e_mx, n * UNIT)
 
         def c_product(u):
             c_acc[u] = psum.tile([P, PACK, UNIT], F32, name="c_acc", bufs=C_BANKS)
-            product(c_acc[u], w1_mx, W1_TILE_ORDER, x_mx[u * UNIT // HALF], u * UNIT % HALF)
+            product(c_acc[u], w1_mx, x_mx[u * UNIT // HALF], u * UNIT % HALF)
 
         def silu(u):
-            filters[u] = keep.tile([P, UNIT, PACK], F32, name=f"filter{u}")
-            nc.scalar.activation(
-                out=filters[u][:], in_=f_acc[u][:].rearrange("p t n -> p n t"), func=mybir.ActivationFunctionType.Silu
-            )
+            if u < 2:
+                filters[u] = w1_raw[1][:, 2 * u : 2 * u + 2, :].rearrange("p j (n t) -> p (j n) t", t=PACK)
+            else:
+                filters[u] = keep.tile([P, UNIT, PACK], F32, name=f"filter{u}")[:]
+            nc.scalar.activation(out=filters[u], in_=f_acc[u][:].rearrange("p t n -> p n t"), func=ACT.Silu)
 
         def z_tile(group):
             if group == Z_GROUPS[-2]:
                 return w2_woven.rearrange("p (n t) -> p n t", t=PACK)
             tag = "e_raw1" if group == Z_GROUPS[0] else ""
-            return keep.tile([P, len(group) * UNIT, PACK], BF16, align_bytes=64, name=f"z_woven{group[0]}", tag=tag)
+            return keep.tile([P, len(group) * UNIT, PACK], BF16, align_bytes=64, name=f"z_woven{group[0]}", tag=tag)[:]
 
         def multiply(u):
             group = [g for g in Z_GROUPS if u in g][0]
@@ -162,14 +168,14 @@ def tile_picked_schnet_silu_e_kernel(tc, xT, eT, w1, w3, w2, offs, out):
             nc.vector.tensor_tensor(
                 out=z_woven[group][:, first : first + UNIT, :],
                 in0=c_acc[u][:].rearrange("p t n -> p n t"),
-                in1=filters[u][:],
+                in1=filters[u],
                 op=mybir.AluOpType.mult,
             )
             if u + C_BANKS < UNITS:
                 c_product(u + C_BANKS)
 
         def quantize_z(group, codes_tag=""):
-            z_mx[group] = quantize_whole(f"z{group[0]}", z_woven[group][:].rearrange("p n t -> p (n t)"), codes_tag)
+            z_mx[group] = quantize_whole(f"z{group[0]}", z_woven[group].rearrange("p n t -> p (n t)"), codes_tag)
 
         result = keep.tile([P, EDGES], F32, name="result")
 
@@ -183,63 +189,66 @@ def tile_picked_schnet_silu_e_kernel(tc, xT, eT, w1, w3, w2, offs, out):
                 last = (group[-1] + 1) * UNIT
                 nc.sync.dma_start(out=out[:, first:last], in_=result[:, first:last])
 
+        entries = [offsets[:, h * HALF // 16 : (h + 1) * HALF // 16] for h in range(2)]
         picked = keep.tile([P, 2, EDGES], F32, name="picked")
+        picked_late = keep.tile([P, 2, HALF], F32, name="picked_late")
         for j in range(2):
             nc.vector.tensor_copy(picked[:, j, :], first_planes[:, j, :].indirect(offsets[:]))
         for h in range(2):
             nc.scalar.copy(
                 out=x_woven[h][:, :, 0:2], in_=picked[:, :, h * HALF : (h + 1) * HALF].rearrange("p j n -> p n j")
             )
-        for j in range(2, PACK):
-            for h in range(2):
-                entries = offsets[:, h * HALF // 16 : (h + 1) * HALF // 16]
-                nc.vector.tensor_copy(x_woven[h][:, :, j], planes[j][:].indirect(entries))
-
-        weave_dealt(nc.scalar.copy, w3_woven, w3_raw, slice(0, PACK), slice(0, P))
+        nc.vector.tensor_copy(x_woven[0][:, :, 2], planes[2][:].indirect(entries[0]))
+        nc.vector.tensor_copy(picked_late[:, 0, :], planes[2][:].indirect(entries[1]))
+        nc.vector.tensor_copy(x_woven[0][:, :, 3], planes[3][:].indirect(entries[0]))
+        nc.scalar.activation(picked_late[:, 1, :], planes[3][:].indirect(entries[1]), ACT.Copy)
+        nc.scalar.copy(out=x_woven[1][:, :, 2:4], in_=picked_late[:].rearrange("p j n -> p n j"))
         x_mx[0] = quantize_whole("x0", x_woven[0][:].rearrange("p n j -> p (n j)"))
-        tensor_warm = psum.tile([P, HALF], F32, name="out_acc", bufs=OUT_BANKS)
-        for warm_pass in range(WARM_PASSES):
-            matmul(tensor_warm[:], x_mx[0], slice(0, P), x_mx[0], slice(0, HALF))
-        weave(nc.vector.tensor_copy, e_woven[0], e_raw[0], slice(0, VECTOR_EDGES[0]))
-        weave(nc.scalar.copy, e_woven[0], e_raw[0], slice(VECTOR_EDGES[0], CHUNK))
-        x_mx[1] = quantize_whole("x1", x_woven[1][:].rearrange("p n j -> p (n j)"))
-        w3_mx = quantize_whole("w3", w3_woven[:])
-        e_mx[0] = quantize_whole("e0", e_woven[0])
 
-        weave_dealt(nc.scalar.copy, w1_woven, w1_raw, slice(3, 4), slice(0, P))
-        weave_dealt(nc.vector.tensor_copy, w1_woven, w1_raw, slice(0, 2), slice(0, P))
-        weave_dealt(nc.vector.tensor_copy, w1_woven, w1_raw, slice(2, 3), slice(0, P // 2))
-        weave_dealt(nc.scalar.copy, w1_woven, w1_raw, slice(2, 3), slice(P // 2, P))
-        f_products(0)
+        weave_dealt(nc.vector.tensor_copy, w3_woven, w3_raw, slice(0, 2), slice(0, P))
+        weave_dealt(nc.vector.tensor_copy, w3_woven, w3_raw, slice(2, 3), slice(0, P))
+        weave_dealt(nc.scalar.copy, w3_woven, w3_raw, slice(3, 4), slice(0, P))
+        w3_mx = mx_tiles("w3", HIDDEN)
+        for first in (0, 2 * P):
+            quantize(w3_mx, slice(first, first + 2 * P), w3_woven[:, first * PACK : (first + 2 * P) * PACK])
+        x_mx[1] = quantize_whole("x1", x_woven[1][:].rearrange("p n j -> p (n j)"), "w3_raw")
+        weave_shared(e_woven[0], e_raw[0], 0, 0)
         w1_mx = mx_tiles("w1", HIDDEN)
-        for first, last in ((3, 4), (0, 2), (2, 3)):
-            quantize(w1_mx, slice(first * P, last * P), w1_woven[:, first * P * PACK : last * P * PACK])
+        for h in range(2):
+            first = h * P // 2
+            weave_dealt(nc.vector.tensor_copy, w1_woven, w1_raw[h], slice(0, 2), slice(0, P // 2), first)
+            if h == 0:
+                weave_dealt(nc.vector.tensor_copy, w1_woven, w1_raw[h], slice(2, 3), slice(0, P // 2), first)
+                weave_dealt(nc.scalar.copy, w1_woven, w1_raw[h], slice(3, 4), slice(0, P // 2), first)
+                quantize_e(0)
+            else:
+                weave_dealt(nc.scalar.copy, w1_woven, w1_raw[h], slice(2, 4), slice(0, P // 2), first)
+            for t in (0, 1, 3, 2) if h == 0 else (2, 3, 0, 1):
+                at = t * P + first
+                quantize(w1_mx, slice(at, at + P // 2), w1_woven[:, at * PACK : (at + P // 2) * PACK])
         for u in range(C_BANKS):
             c_product(u)
         silu(0)
-        weave(nc.vector.tensor_copy, e_woven[1], e_raw[1], slice(0, VECTOR_EDGES[1]))
-        weave(nc.scalar.copy, e_woven[1], e_raw[1], slice(VECTOR_EDGES[1], CHUNK))
+        weave(nc.vector.tensor_copy, e_woven[1], e_raw[1], slice(0, 2 * UNIT))
         silu(1)
-        e_mx[1] = quantize_whole("e1", e_woven[1])
-        f_products(1)
+        quantize_e(1)
 
-        for k in range(CHUNKS - 1):
-            ahead = k + 2
-            if ahead < CHUNKS:
-                weave_late(e_woven[ahead], e_raw[ahead], GPSIMD_COLUMNS[k])
+        for turn in range(3):
+            ahead = turn + 2
+            if ahead < len(PIECES):
+                weave_shared(e_woven[ahead], e_raw[ahead], GPSIMD_COLUMNS[turn], 0)
             else:
-                weave_late(w2_woven, w2_raw, GPSIMD_COLUMNS[k])
-            multiply(2 * k)
-            multiply(2 * k + 1)
-            silu(2 * k + 2)
-            silu(2 * k + 3)
-            if ahead < CHUNKS:
-                e_mx[ahead] = quantize_whole(f"e{ahead}", e_woven[ahead])
-                f_products(ahead)
-                quantize_z(Z_GROUPS[k], f"e_raw{ahead}")
+                weave_shared(w2_woven, w2_raw, GPSIMD_COLUMNS[turn], 0)
+            multiply(2 * turn)
+            multiply(2 * turn + 1)
+            silu(2 * turn + 2)
+            silu(2 * turn + 3)
+            if ahead < len(PIECES):
+                quantize_e(ahead)
+                quantize_z(Z_GROUPS[turn], f"e_raw{ahead}")
             else:
                 w2_mx = quantize_whole("w2", w2_woven)
-                quantize_z(Z_GROUPS[k])
+                quantize_z(Z_GROUPS[turn])
         for group in Z_GROUPS[-2:]:
             multiply(group[0])
         for group in Z_GROUPS[-2:]:

@@ -34,7 +34,7 @@ def tile_picked_schnet_silu_e_kernel(tc, xT, eT, w1, w3, w2, offs, out):
         offsets = keep.tile([P, EDGES // 16], U16, name="offsets")
         first_planes = keep.tile([P, 2, ATOMS], F32, name="first_planes")
         planes = {j: keep.tile([P, ATOMS], F32, name=f"plane{j}") for j in range(2, PACK)}
-        w1_raw = [keep.tile([P, PACK, HIDDEN // 2], F32, align_bytes=64, name=f"w1_raw{h}") for h in range(2)]
+        w1_raw = keep.tile([P, PACK, HIDDEN], F32, align_bytes=64, name="w1_raw")
         w3_raw = keep.tile([P, PACK, HIDDEN], F32, align_bytes=64, name="w3_raw")
         w2_raw = keep.tile([P, PACK, OUT_ROWS], F32, name="w2_raw")
         e_raw = [keep.tile([P, PACK, n * UNIT], F32, align_bytes=64, name=f"e_raw{k}") for k, n in enumerate(PIECES)]
@@ -51,8 +51,7 @@ def tile_picked_schnet_silu_e_kernel(tc, xT, eT, w1, w3, w2, offs, out):
         for k, n in enumerate(PIECES):
             nc.sync.dma_start(out=e_raw[k][:], in_=e_rows[:, :, e_first[k] * UNIT : (e_first[k] + n) * UNIT])
             if k == 0:
-                for h in range(2):
-                    nc.sync.dma_start(out=w1_raw[h][:], in_=w1_rows[:, :, h * HIDDEN // 2 : (h + 1) * HIDDEN // 2])
+                nc.sync.dma_start(out=w1_raw[:], in_=w1_rows)
         w2_rows = w2.rearrange("(q t r) c -> r q t c", t=PACK, r=2)
         for r in range(2):
             nc.sync.dma_start(out=w2_raw[r:P:2, :, :], in_=w2_rows[r])
@@ -130,7 +129,7 @@ def tile_picked_schnet_silu_e_kernel(tc, xT, eT, w1, w3, w2, offs, out):
             )
 
         def product(acc, weight, moving, first):
-            for t in (2, 3, 0, 1):
+            for t in (3, 0, 1, 2):
                 matmul(acc[:, t, :], weight, slice(t * P, (t + 1) * P), moving, slice(first, first + UNIT))
 
         x_mx, z_mx = {}, {}
@@ -149,7 +148,7 @@ def tile_picked_schnet_silu_e_kernel(tc, xT, eT, w1, w3, w2, offs, out):
 
         def silu(u):
             if u < 2:
-                filters[u] = w1_raw[1][:, 2 * u : 2 * u + 2, :].rearrange("p j (n t) -> p (j n) t", t=PACK)
+                filters[u] = w1_raw[:, u, :].rearrange("p (n t) -> p n t", t=PACK)
             else:
                 filters[u] = keep.tile([P, UNIT, PACK], F32, name=f"filter{u}")[:]
             nc.scalar.activation(out=filters[u], in_=f_acc[u][:].rearrange("p t n -> p n t"), func=ACT.Silu)
@@ -213,19 +212,14 @@ def tile_picked_schnet_silu_e_kernel(tc, xT, eT, w1, w3, w2, offs, out):
             quantize(w3_mx, slice(first, first + 2 * P), w3_woven[:, first * PACK : (first + 2 * P) * PACK])
         x_mx[1] = quantize_whole("x1", x_woven[1][:].rearrange("p n j -> p (n j)"), "w3_raw")
         weave_shared(e_woven[0], e_raw[0], 0, 0)
+        quantize_e(0)
         w1_mx = mx_tiles("w1", HIDDEN)
-        for h in range(2):
-            first = h * P // 2
-            weave_dealt(nc.vector.tensor_copy, w1_woven, w1_raw[h], slice(0, 2), slice(0, P // 2), first)
-            if h == 0:
-                weave_dealt(nc.vector.tensor_copy, w1_woven, w1_raw[h], slice(2, 3), slice(0, P // 2), first)
-                weave_dealt(nc.scalar.copy, w1_woven, w1_raw[h], slice(3, 4), slice(0, P // 2), first)
-                quantize_e(0)
-            else:
-                weave_dealt(nc.scalar.copy, w1_woven, w1_raw[h], slice(2, 4), slice(0, P // 2), first)
-            for t in (0, 1, 3, 2) if h == 0 else (2, 3, 0, 1):
-                at = t * P + first
-                quantize(w1_mx, slice(at, at + P // 2), w1_woven[:, at * PACK : (at + P // 2) * PACK])
+        weave_dealt(nc.scalar.copy, w1_woven, w1_raw, slice(3, 4), slice(0, P))
+        weave_dealt(nc.vector.tensor_copy, w1_woven, w1_raw, slice(0, 2), slice(0, P))
+        weave_dealt(nc.vector.tensor_copy, w1_woven, w1_raw, slice(2, 3), slice(0, P // 2))
+        weave_dealt(nc.scalar.copy, w1_woven, w1_raw, slice(2, 3), slice(P // 2, P))
+        for first, last in ((3, 4), (0, 2), (2, 3)):
+            quantize(w1_mx, slice(first * P, last * P), w1_woven[:, first * P * PACK : last * P * PACK])
         for u in range(C_BANKS):
             c_product(u)
         silu(0)

@@ -20,7 +20,8 @@ UNIT = 128
 UNITS = EDGES // UNIT
 PIECES = (2, 2, 2, 2)
 C_BANKS, F_BANKS, OUT_BANKS = 3, 2, 3
-GPSIMD_COLUMNS = (64, 104, 88)
+GPSIMD_COLUMNS = (64, 88, 88)
+E3_VECTOR_EDGES = 56
 Z_GROUPS = ((0, 1), (2, 3), (4, 5), (6,), (7,))
 STORE_ENDS = (2, 6, 7, 8)
 
@@ -37,7 +38,12 @@ def tile_picked_schnet_silu_e_kernel(tc, xT, eT, w1, w3, w2, offs, out):
         w1_raw = keep.tile([P, PACK, HIDDEN], F32, align_bytes=64, name="w1_raw")
         w3_raw = keep.tile([P, PACK, HIDDEN], F32, align_bytes=64, name="w3_raw")
         w2_raw = keep.tile([P, PACK, OUT_ROWS], F32, name="w2_raw")
-        e_raw = [keep.tile([P, PACK, n * UNIT], F32, align_bytes=64, name=f"e_raw{k}") for k, n in enumerate(PIECES)]
+        e_raw = {k: keep.tile([P, PACK, 2 * UNIT], F32, align_bytes=64, name=f"e_raw{k}")[:] for k in (0, 2, 3)}
+        chunk = 2 * UNIT * PACK
+        e3_first = 2 * chunk - GPSIMD_COLUMNS[1] * PACK
+        w2_first = e3_first + chunk - GPSIMD_COLUMNS[2] * PACK
+        room = keep.tile([P, w2_first + OUT_ROWS * PACK], BF16, align_bytes=64, name="room")
+        e_raw[1] = room[:, 0 : 2 * chunk].bitcast(F32).rearrange("p (j n) -> p j n", j=PACK)
         e_first = [sum(PIECES[:k]) for k in range(len(PIECES))]
         x_rows = xT.rearrange("(p j) n -> p j n", j=PACK)
         e_rows = eT.rearrange("(p j) n -> p j n", j=PACK)
@@ -49,7 +55,7 @@ def tile_picked_schnet_silu_e_kernel(tc, xT, eT, w1, w3, w2, offs, out):
         nc.sync.dma_start(out=w3_raw[:], in_=w3.rearrange("(p j) c -> p j c", j=PACK))
         w1_rows = w1.rearrange("(p j) c -> p j c", j=PACK)
         for k, n in enumerate(PIECES):
-            nc.sync.dma_start(out=e_raw[k][:], in_=e_rows[:, :, e_first[k] * UNIT : (e_first[k] + n) * UNIT])
+            nc.sync.dma_start(out=e_raw[k], in_=e_rows[:, :, e_first[k] * UNIT : (e_first[k] + n) * UNIT])
             if k == 0:
                 nc.sync.dma_start(out=w1_raw[:], in_=w1_rows)
         w2_rows = w2.rearrange("(q t r) c -> r q t c", t=PACK, r=2)
@@ -64,12 +70,10 @@ def tile_picked_schnet_silu_e_kernel(tc, xT, eT, w1, w3, w2, offs, out):
         w1_woven = keep.tile([P, HIDDEN * PACK], BF16, align_bytes=64, name="w1_woven")
         w3_woven = keep.tile([P, HIDDEN * PACK], BF16, align_bytes=64, name="w3_woven")
         early = [keep.tile([P, 2 * UNIT * PACK], BF16, align_bytes=64, name="e_woven0")]
-        late_starts = [0]
-        for columns in GPSIMD_COLUMNS:
-            late_starts.append(late_starts[-1] + (2 * UNIT - columns) * PACK)
-        late = keep.tile([P, late_starts[-1] + OUT_ROWS * PACK], BF16, align_bytes=64, name="late")
-        e_woven = [t[:] for t in early] + [late[:, first : first + 2 * UNIT * PACK] for first in late_starts[:-1]]
-        w2_woven = late[:, late_starts[-1] : late_starts[-1] + OUT_ROWS * PACK]
+        e2_first = chunk - GPSIMD_COLUMNS[0] * PACK
+        late = keep.tile([P, e2_first + chunk], BF16, align_bytes=64, name="late")
+        e_woven = [early[0][:], late[:, 0:chunk], late[:, e2_first:], room[:, e3_first : e3_first + chunk]]
+        w2_woven = room[:, w2_first:]
 
         def weave(copy, woven, raw, columns):
             pairs = slice(columns.start // 2, columns.stop // 2)
@@ -156,8 +160,9 @@ def tile_picked_schnet_silu_e_kernel(tc, xT, eT, w1, w3, w2, offs, out):
         def z_tile(group):
             if group == Z_GROUPS[-2]:
                 return w2_woven.rearrange("p (n t) -> p n t", t=PACK)
-            tag = "e_raw1" if group == Z_GROUPS[0] else ""
-            return keep.tile([P, len(group) * UNIT, PACK], BF16, align_bytes=64, name=f"z_woven{group[0]}", tag=tag)[:]
+            if group == Z_GROUPS[0]:
+                return room[:, chunk : 2 * chunk].rearrange("p (n t) -> p n t", t=PACK)
+            return keep.tile([P, len(group) * UNIT, PACK], BF16, align_bytes=64, name=f"z_woven{group[0]}")[:]
 
         def multiply(u):
             group = [g for g in Z_GROUPS if u in g][0]
@@ -230,7 +235,7 @@ def tile_picked_schnet_silu_e_kernel(tc, xT, eT, w1, w3, w2, offs, out):
         for turn in range(3):
             ahead = turn + 2
             if ahead < len(PIECES):
-                weave_shared(e_woven[ahead], e_raw[ahead], GPSIMD_COLUMNS[turn], 0)
+                weave_shared(e_woven[ahead], e_raw[ahead], GPSIMD_COLUMNS[turn], E3_VECTOR_EDGES * turn)
             else:
                 weave_shared(w2_woven, w2_raw, GPSIMD_COLUMNS[turn], 0)
             multiply(2 * turn)

@@ -90,7 +90,7 @@ def tile_picked_schnet_silu_e_kernel(tc, xT, eT, w1, w3, w2, offs, out):
                 in_=raw[:].rearrange("p j (q t r) -> p q t j r", t=PACK, r=2)[:, pairs, tiles],
             )
 
-        def weave_shared(woven, raw, gpsimd_columns, vector_columns):
+        def weave_shared(woven, raw, gpsimd_columns, vector_columns, scalar_cuts):
             width = raw.shape[2]
             if gpsimd_columns:
                 nc.gpsimd.tensor_scalar(
@@ -101,8 +101,9 @@ def tile_picked_schnet_silu_e_kernel(tc, xT, eT, w1, w3, w2, offs, out):
                     op0=mybir.AluOpType.mult,
                     op1=mybir.AluOpType.add,
                 )
-            if gpsimd_columns + vector_columns < width:
-                weave(nc.scalar.copy, woven, raw, slice(gpsimd_columns, width - vector_columns))
+            cuts = [gpsimd_columns] + scalar_cuts + [width - vector_columns]
+            for first, last in zip(cuts, cuts[1:]):
+                weave(nc.scalar.copy, woven, raw, slice(first, last))
             if vector_columns:
                 weave(nc.vector.tensor_copy, woven, raw, slice(width - vector_columns, width))
 
@@ -133,18 +134,27 @@ def tile_picked_schnet_silu_e_kernel(tc, xT, eT, w1, w3, w2, offs, out):
             )
 
         def product(acc, weight, moving, first):
-            for t in (3, 0, 1, 2):
+            for t in range(PACK):
                 matmul(acc[:, t, :], weight, slice(t * P, (t + 1) * P), moving, slice(first, first + UNIT))
 
-        x_mx, z_mx = {}, {}
+        x_mx, e_mx, z_mx = {}, {}, {}
         c_acc, f_acc, filters, z_woven = {}, {}, {}, {}
 
+        def f_product(u):
+            f_acc[u] = psum.tile([P, PACK, UNIT], F32, name="f_acc", bufs=F_BANKS)
+            product(f_acc[u], w3_mx, e_mx[u // 2], u % 2 * UNIT)
+
         def quantize_e(k):
-            e_mx = quantize_whole(f"e{k}", e_woven[k])
-            for n in range(PIECES[k]):
-                u = e_first[k] + n
-                f_acc[u] = psum.tile([P, PACK, UNIT], F32, name="f_acc", bufs=F_BANKS)
-                product(f_acc[u], w3_mx, e_mx, n * UNIT)
+            e_mx[k] = quantize_whole(f"e{k}", e_woven[k])
+            f_product(2 * k)
+            f_product(2 * k + 1)
+
+        def quantize_e_unit(u):
+            if u % 2 == 0:
+                e_mx[u // 2] = mx_tiles(f"e{u // 2}", 2 * UNIT)
+            edges = slice(u % 2 * UNIT, (u % 2 + 1) * UNIT)
+            quantize(e_mx[u // 2], edges, e_woven[u // 2][:, edges.start * PACK : edges.stop * PACK])
+            f_product(u)
 
         def c_product(u):
             c_acc[u] = psum.tile([P, PACK, UNIT], F32, name="c_acc", bufs=C_BANKS)
@@ -216,14 +226,13 @@ def tile_picked_schnet_silu_e_kernel(tc, xT, eT, w1, w3, w2, offs, out):
         for first in (0, 2 * P):
             quantize(w3_mx, slice(first, first + 2 * P), w3_woven[:, first * PACK : (first + 2 * P) * PACK])
         x_mx[1] = quantize_whole("x1", x_woven[1][:].rearrange("p n j -> p (n j)"), "w3_raw")
-        weave_shared(e_woven[0], e_raw[0], 0, 0)
+        weave_shared(e_woven[0], e_raw[0], 0, 0, [])
         quantize_e(0)
         w1_mx = mx_tiles("w1", HIDDEN)
-        weave_dealt(nc.scalar.copy, w1_woven, w1_raw, slice(3, 4), slice(0, P))
         weave_dealt(nc.vector.tensor_copy, w1_woven, w1_raw, slice(0, 2), slice(0, P))
-        weave_dealt(nc.vector.tensor_copy, w1_woven, w1_raw, slice(2, 3), slice(0, P // 2))
-        weave_dealt(nc.scalar.copy, w1_woven, w1_raw, slice(2, 3), slice(P // 2, P))
-        for first, last in ((3, 4), (0, 2), (2, 3)):
+        weave_dealt(nc.vector.tensor_copy, w1_woven, w1_raw, slice(2, 4), slice(0, P // 4))
+        weave_dealt(nc.scalar.copy, w1_woven, w1_raw, slice(2, 4), slice(P // 4, P))
+        for first, last in ((0, 2), (2, 4)):
             quantize(w1_mx, slice(first * P, last * P), w1_woven[:, first * P * PACK : last * P * PACK])
         for u in range(C_BANKS):
             c_product(u)
@@ -235,14 +244,18 @@ def tile_picked_schnet_silu_e_kernel(tc, xT, eT, w1, w3, w2, offs, out):
         for turn in range(3):
             ahead = turn + 2
             if ahead < len(PIECES):
-                weave_shared(e_woven[ahead], e_raw[ahead], GPSIMD_COLUMNS[turn], E3_VECTOR_EDGES * turn)
+                weave_shared(e_woven[ahead], e_raw[ahead], GPSIMD_COLUMNS[turn], E3_VECTOR_EDGES * turn, [UNIT] * (1 - turn))
             else:
-                weave_shared(w2_woven, w2_raw, GPSIMD_COLUMNS[turn], 0)
+                weave_shared(w2_woven, w2_raw, GPSIMD_COLUMNS[turn], 0, [])
             multiply(2 * turn)
             multiply(2 * turn + 1)
             silu(2 * turn + 2)
             silu(2 * turn + 3)
-            if ahead < len(PIECES):
+            if turn == 0:
+                quantize_e_unit(2 * ahead)
+                quantize_z(Z_GROUPS[turn], f"e_raw{ahead}")
+                quantize_e_unit(2 * ahead + 1)
+            elif ahead < len(PIECES):
                 quantize_e(ahead)
                 quantize_z(Z_GROUPS[turn], f"e_raw{ahead}")
             else:

@@ -20,8 +20,8 @@ UNIT = 128
 UNITS = EDGES // UNIT
 PIECES = (2, 2, 2, 2)
 C_BANKS, F_BANKS, OUT_BANKS = 3, 2, 3
-GPSIMD_COLUMNS = (64, 88, 88)
-E3_VECTOR_EDGES = 56
+GPSIMD_COLUMNS = (72, 96, 104)
+E3_VECTOR_EDGES = 32
 Z_GROUPS = ((0, 1), (2, 3), (4, 5), (6,), (7,))
 STORE_ENDS = (2, 6, 7, 8)
 

@@ -17,11 +17,12 @@ FLOPS = 2 * (2 * K * HIDDEN * EDGES) + 2 * HIDDEN * OUT_ROWS * EDGES
 
 HALF = EDGES // 2
 UNIT = 128
+CHUNK = 2 * UNIT
 UNITS = EDGES // UNIT
-PIECES = (2, 2, 2, 2)
+CHUNKS = EDGES // CHUNK
+WOVEN_CHUNK = CHUNK * PACK
 C_BANKS, F_BANKS, OUT_BANKS = 3, 2, 3
-GPSIMD_COLUMNS = (72, 96, 104)
-E3_VECTOR_EDGES = 32
+GPSIMD_COLUMNS = (80, 112, 96)
 Z_GROUPS = ((0, 1), (2, 3), (4, 5), (6,), (7,))
 STORE_ENDS = (2, 6, 7, 8)
 
@@ -38,26 +39,25 @@ def tile_picked_schnet_silu_e_kernel(tc, xT, eT, w1, w3, w2, offs, out):
         w1_raw = keep.tile([P, PACK, HIDDEN], F32, align_bytes=64, name="w1_raw")
         w3_raw = keep.tile([P, PACK, HIDDEN], F32, align_bytes=64, name="w3_raw")
         w2_raw = keep.tile([P, PACK, OUT_ROWS], F32, name="w2_raw")
-        e_raw = {k: keep.tile([P, PACK, 2 * UNIT], F32, align_bytes=64, name=f"e_raw{k}")[:] for k in (0, 2, 3)}
-        chunk = 2 * UNIT * PACK
-        e3_first = 2 * chunk - GPSIMD_COLUMNS[1] * PACK
-        w2_first = e3_first + chunk - GPSIMD_COLUMNS[2] * PACK
-        room = keep.tile([P, w2_first + OUT_ROWS * PACK], BF16, align_bytes=64, name="room")
-        e_raw[1] = room[:, 0 : 2 * chunk].bitcast(F32).rearrange("p (j n) -> p j n", j=PACK)
-        e_first = [sum(PIECES[:k]) for k in range(len(PIECES))]
+        e_raw = {k: keep.tile([P, PACK, CHUNK], F32, align_bytes=64, name=f"e_raw{k}")[:] for k in (0, 2, 3)}
+        e3_first = GPSIMD_COLUMNS[1] * PACK
+        relay = keep.tile([P, 2 * WOVEN_CHUNK], BF16, align_bytes=64, name="relay")
+        e_raw[1] = relay[:].bitcast(F32).rearrange("p (j n) -> p j n", j=PACK)
         x_rows = xT.rearrange("(p j) n -> p j n", j=PACK)
         e_rows = eT.rearrange("(p j) n -> p j n", j=PACK)
+
+        def load_e(k):
+            nc.sync.dma_start(out=e_raw[k], in_=e_rows[:, :, k * CHUNK : (k + 1) * CHUNK])
 
         nc.sync.dma_start(out=first_planes[:], in_=x_rows[:, 0:2, :])
         nc.sync.dma_start(offsets[:], offs)
         for j in range(2, PACK):
             nc.sync.dma_start(out=planes[j][:], in_=x_rows[:, j, :])
         nc.sync.dma_start(out=w3_raw[:], in_=w3.rearrange("(p j) c -> p j c", j=PACK))
-        w1_rows = w1.rearrange("(p j) c -> p j c", j=PACK)
-        for k, n in enumerate(PIECES):
-            nc.sync.dma_start(out=e_raw[k], in_=e_rows[:, :, e_first[k] * UNIT : (e_first[k] + n) * UNIT])
-            if k == 0:
-                nc.sync.dma_start(out=w1_raw[:], in_=w1_rows)
+        load_e(0)
+        nc.sync.dma_start(out=w1_raw[:], in_=w1.rearrange("(p j) c -> p j c", j=PACK))
+        for k in range(1, CHUNKS):
+            load_e(k)
         w2_rows = w2.rearrange("(q t r) c -> r q t c", t=PACK, r=2)
         for r in range(2):
             nc.sync.dma_start(out=w2_raw[r:P:2, :, :], in_=w2_rows[r])
@@ -69,43 +69,43 @@ def tile_picked_schnet_silu_e_kernel(tc, xT, eT, w1, w3, w2, offs, out):
         x_woven = [keep.tile([P, HALF, PACK], BF16, align_bytes=64, name=f"x_woven{h}") for h in range(2)]
         w1_woven = keep.tile([P, HIDDEN * PACK], BF16, align_bytes=64, name="w1_woven")
         w3_woven = keep.tile([P, HIDDEN * PACK], BF16, align_bytes=64, name="w3_woven")
-        early = [keep.tile([P, 2 * UNIT * PACK], BF16, align_bytes=64, name="e_woven0")]
-        e2_first = chunk - GPSIMD_COLUMNS[0] * PACK
-        late = keep.tile([P, e2_first + chunk], BF16, align_bytes=64, name="late")
-        e_woven = [early[0][:], late[:, 0:chunk], late[:, e2_first:], room[:, e3_first : e3_first + chunk]]
-        w2_woven = room[:, w2_first:]
+        e0_woven = keep.tile([P, WOVEN_CHUNK], BF16, align_bytes=64, name="e0_woven")
+        e2_first = WOVEN_CHUNK - GPSIMD_COLUMNS[0] * PACK
+        e12_woven = keep.tile([P, e2_first + WOVEN_CHUNK], BF16, align_bytes=64, name="e12_woven")
+        e_woven = [
+            e0_woven[:],
+            e12_woven[:, e2_first:],
+            e12_woven[:, 0:WOVEN_CHUNK],
+            relay[:, e3_first : e3_first + WOVEN_CHUNK],
+        ]
+        z1_first = (OUT_ROWS - GPSIMD_COLUMNS[2]) * PACK
+        w2_z1 = keep.tile([P, z1_first + WOVEN_CHUNK], BF16, align_bytes=64, name="w2_z1")
+        w2_woven = w2_z1[:, 0 : OUT_ROWS * PACK]
 
         def weave(copy, woven, raw, columns):
             pairs = slice(columns.start // 2, columns.stop // 2)
             copy(
                 out=woven.rearrange("p (c r j) -> p c j r", r=2, j=PACK)[:, pairs],
-                in_=raw[:].rearrange("p j (c r) -> p c j r", r=2)[:, pairs],
+                in_=raw.rearrange("p j (c r) -> p c j r", r=2)[:, pairs],
             )
 
-        def weave_dealt(copy, woven, raw, tiles, columns, first=0):
+        def weave_dealt(copy, woven, raw, tiles, columns):
             pairs = slice(columns.start // 2, columns.stop // 2)
-            places = slice((first + columns.start) // 2, (first + columns.stop) // 2)
             copy(
-                out=woven[:].rearrange("p (t q r j) -> p q t j r", t=PACK, r=2, j=PACK)[:, places, tiles],
+                out=woven[:].rearrange("p (t q r j) -> p q t j r", t=PACK, r=2, j=PACK)[:, pairs, tiles],
                 in_=raw[:].rearrange("p j (q t r) -> p q t j r", t=PACK, r=2)[:, pairs, tiles],
             )
 
-        def weave_shared(woven, raw, gpsimd_columns, vector_columns, scalar_cuts):
-            width = raw.shape[2]
-            if gpsimd_columns:
-                nc.gpsimd.tensor_scalar(
-                    out=woven.rearrange("p (c j) -> p c j", j=PACK)[:, 0:gpsimd_columns],
-                    in0=raw[:].rearrange("p j c -> p c j")[:, 0:gpsimd_columns],
-                    scalar1=1.0,
-                    scalar2=0.0,
-                    op0=mybir.AluOpType.mult,
-                    op1=mybir.AluOpType.add,
-                )
-            cuts = [gpsimd_columns] + scalar_cuts + [width - vector_columns]
-            for first, last in zip(cuts, cuts[1:]):
-                weave(nc.scalar.copy, woven, raw, slice(first, last))
-            if vector_columns:
-                weave(nc.vector.tensor_copy, woven, raw, slice(width - vector_columns, width))
+        def weave_gpsimd(woven, raw, columns):
+            first_pair = (raw.shape[2] - columns) // 2
+            nc.gpsimd.tensor_scalar(
+                out=woven.rearrange("p (c r j) -> p c j r", r=2, j=PACK)[:, first_pair:],
+                in0=raw.rearrange("p j (c r) -> p c j r", r=2)[:, first_pair:],
+                scalar1=1.0,
+                scalar2=0.0,
+                op0=mybir.AluOpType.mult,
+                op1=mybir.AluOpType.add,
+            )
 
         def mx_tiles(name, width, codes_tag=""):
             codes = keep.tile([P, width], U32, align_bytes=64, name=f"{name}_codes", tag=codes_tag)
@@ -114,12 +114,22 @@ def tile_picked_schnet_silu_e_kernel(tc, xT, eT, w1, w3, w2, offs, out):
 
         def quantize(operand, columns, woven):
             codes, scales = operand
-            nc.vector.quantize_mx(out=codes[:, columns].bitcast(FP8X4), scales=scales[:, columns], in_=woven)
+            nc.vector.quantize_mx(
+                out=codes[:, columns].bitcast(FP8X4),
+                scales=scales[:, columns],
+                in_=woven[:, columns.start * PACK : columns.stop * PACK],
+            )
 
         def quantize_whole(name, woven, codes_tag=""):
             width = woven.shape[1] // PACK
             operand = mx_tiles(name, width, codes_tag)
             quantize(operand, slice(0, width), woven)
+            return operand
+
+        def quantize_weight(name, woven):
+            operand = mx_tiles(name, HIDDEN)
+            for first in (0, 2 * P):
+                quantize(operand, slice(first, first + 2 * P), woven)
             return operand
 
         def matmul(acc, stationary, stationary_columns, moving, moving_columns):
@@ -142,7 +152,11 @@ def tile_picked_schnet_silu_e_kernel(tc, xT, eT, w1, w3, w2, offs, out):
 
         def f_product(u):
             f_acc[u] = psum.tile([P, PACK, UNIT], F32, name="f_acc", bufs=F_BANKS)
-            product(f_acc[u], w3_mx, e_mx[u // 2], u % 2 * UNIT)
+            product(f_acc[u], w3_mx, e_mx[u * UNIT // CHUNK], u * UNIT % CHUNK)
+
+        def c_product(u):
+            c_acc[u] = psum.tile([P, PACK, UNIT], F32, name="c_acc", bufs=C_BANKS)
+            product(c_acc[u], w1_mx, x_mx[u * UNIT // HALF], u * UNIT % HALF)
 
         def quantize_e(k):
             e_mx[k] = quantize_whole(f"e{k}", e_woven[k])
@@ -150,34 +164,30 @@ def tile_picked_schnet_silu_e_kernel(tc, xT, eT, w1, w3, w2, offs, out):
             f_product(2 * k + 1)
 
         def quantize_e_unit(u):
-            if u % 2 == 0:
-                e_mx[u // 2] = mx_tiles(f"e{u // 2}", 2 * UNIT)
-            edges = slice(u % 2 * UNIT, (u % 2 + 1) * UNIT)
-            quantize(e_mx[u // 2], edges, e_woven[u // 2][:, edges.start * PACK : edges.stop * PACK])
+            k, first = divmod(u * UNIT, CHUNK)
+            quantize(e_mx[k], slice(first, first + UNIT), e_woven[k])
             f_product(u)
 
-        def c_product(u):
-            c_acc[u] = psum.tile([P, PACK, UNIT], F32, name="c_acc", bufs=C_BANKS)
-            product(c_acc[u], w1_mx, x_mx[u * UNIT // HALF], u * UNIT % HALF)
-
         def silu(u):
-            if u < 2:
+            if u * UNIT < CHUNK:
                 filters[u] = w1_raw[:, u, :].rearrange("p (n t) -> p n t", t=PACK)
             else:
                 filters[u] = keep.tile([P, UNIT, PACK], F32, name=f"filter{u}")[:]
             nc.scalar.activation(out=filters[u], in_=f_acc[u][:].rearrange("p t n -> p n t"), func=ACT.Silu)
 
-        def z_tile(group):
+        def z_place(group):
             if group == Z_GROUPS[-2]:
                 return w2_woven.rearrange("p (n t) -> p n t", t=PACK)
+            if group == Z_GROUPS[1]:
+                return w2_z1[:, z1_first:].rearrange("p (n t) -> p n t", t=PACK)
             if group == Z_GROUPS[0]:
-                return room[:, chunk : 2 * chunk].rearrange("p (n t) -> p n t", t=PACK)
+                return relay[:, WOVEN_CHUNK : 2 * WOVEN_CHUNK].rearrange("p (n t) -> p n t", t=PACK)
             return keep.tile([P, len(group) * UNIT, PACK], BF16, align_bytes=64, name=f"z_woven{group[0]}")[:]
 
         def multiply(u):
             group = [g for g in Z_GROUPS if u in g][0]
             if u == group[0]:
-                z_woven[group] = z_tile(group)
+                z_woven[group] = z_place(group)
             first = (u - group[0]) * UNIT
             nc.vector.tensor_tensor(
                 out=z_woven[group][:, first : first + UNIT, :],
@@ -187,6 +197,12 @@ def tile_picked_schnet_silu_e_kernel(tc, xT, eT, w1, w3, w2, offs, out):
             )
             if u + C_BANKS < UNITS:
                 c_product(u + C_BANKS)
+
+        def multiply_pair(k):
+            multiply(2 * k)
+            multiply(2 * k + 1)
+            silu(2 * k + 2)
+            silu(2 * k + 3)
 
         def quantize_z(group, codes_tag=""):
             z_mx[group] = quantize_whole(f"z{group[0]}", z_woven[group].rearrange("p n t -> p (n t)"), codes_tag)
@@ -222,45 +238,44 @@ def tile_picked_schnet_silu_e_kernel(tc, xT, eT, w1, w3, w2, offs, out):
         weave_dealt(nc.vector.tensor_copy, w3_woven, w3_raw, slice(0, 2), slice(0, P))
         weave_dealt(nc.vector.tensor_copy, w3_woven, w3_raw, slice(2, 3), slice(0, P))
         weave_dealt(nc.scalar.copy, w3_woven, w3_raw, slice(3, 4), slice(0, P))
-        w3_mx = mx_tiles("w3", HIDDEN)
-        for first in (0, 2 * P):
-            quantize(w3_mx, slice(first, first + 2 * P), w3_woven[:, first * PACK : (first + 2 * P) * PACK])
+        w3_mx = quantize_weight("w3", w3_woven)
         x_mx[1] = quantize_whole("x1", x_woven[1][:].rearrange("p n j -> p (n j)"), "w3_raw")
-        weave_shared(e_woven[0], e_raw[0], 0, 0, [])
+        weave(nc.scalar.copy, e_woven[0], e_raw[0], slice(0, CHUNK))
         quantize_e(0)
-        w1_mx = mx_tiles("w1", HIDDEN)
         weave_dealt(nc.vector.tensor_copy, w1_woven, w1_raw, slice(0, 2), slice(0, P))
         weave_dealt(nc.vector.tensor_copy, w1_woven, w1_raw, slice(2, 4), slice(0, P // 4))
         weave_dealt(nc.scalar.copy, w1_woven, w1_raw, slice(2, 4), slice(P // 4, P))
-        for first, last in ((0, 2), (2, 4)):
-            quantize(w1_mx, slice(first * P, last * P), w1_woven[:, first * P * PACK : last * P * PACK])
+        w1_mx = quantize_weight("w1", w1_woven)
         for u in range(C_BANKS):
             c_product(u)
         silu(0)
-        weave(nc.vector.tensor_copy, e_woven[1], e_raw[1], slice(0, 2 * UNIT))
+        weave(nc.vector.tensor_copy, e_woven[1], e_raw[1], slice(0, CHUNK))
         silu(1)
         quantize_e(1)
 
-        for turn in range(3):
-            ahead = turn + 2
-            if ahead < len(PIECES):
-                weave_shared(e_woven[ahead], e_raw[ahead], GPSIMD_COLUMNS[turn], E3_VECTOR_EDGES * turn, [UNIT] * (1 - turn))
-            else:
-                weave_shared(w2_woven, w2_raw, GPSIMD_COLUMNS[turn], 0, [])
-            multiply(2 * turn)
-            multiply(2 * turn + 1)
-            silu(2 * turn + 2)
-            silu(2 * turn + 3)
-            if turn == 0:
-                quantize_e_unit(2 * ahead)
-                quantize_z(Z_GROUPS[turn], f"e_raw{ahead}")
-                quantize_e_unit(2 * ahead + 1)
-            elif ahead < len(PIECES):
-                quantize_e(ahead)
-                quantize_z(Z_GROUPS[turn], f"e_raw{ahead}")
-            else:
-                w2_mx = quantize_whole("w2", w2_woven)
-                quantize_z(Z_GROUPS[turn])
+        weave_gpsimd(e_woven[2], e_raw[2], GPSIMD_COLUMNS[0])
+        weave(nc.scalar.copy, e_woven[2], e_raw[2], slice(0, UNIT))
+        weave(nc.scalar.copy, e_woven[2], e_raw[2], slice(UNIT, CHUNK - GPSIMD_COLUMNS[0]))
+        multiply_pair(0)
+        e_mx[2] = mx_tiles("e2", CHUNK)
+        quantize_e_unit(4)
+        quantize_z(Z_GROUPS[0], "e_raw2")
+        quantize_e_unit(5)
+
+        weave_gpsimd(e_woven[3], e_raw[3], GPSIMD_COLUMNS[1])
+        weave(nc.scalar.copy, e_woven[3], e_raw[3], slice(0, CHUNK - GPSIMD_COLUMNS[1]))
+        multiply_pair(1)
+        e_mx[3] = mx_tiles("e3", CHUNK)
+        quantize_e_unit(6)
+        quantize_z(Z_GROUPS[1], "e_raw3")
+        quantize_e_unit(7)
+
+        weave_gpsimd(w2_woven, w2_raw[:], GPSIMD_COLUMNS[2])
+        weave(nc.scalar.copy, w2_woven, w2_raw[:], slice(0, OUT_ROWS - GPSIMD_COLUMNS[2]))
+        multiply_pair(2)
+        w2_mx = quantize_whole("w2", w2_woven)
+        quantize_z(Z_GROUPS[2])
+
         for group in Z_GROUPS[-2:]:
             multiply(group[0])
         for group in Z_GROUPS[-2:]:

from contextlib import ExitStack

import concourse.mybir as mybir

F32 = mybir.dt.float32
BF16 = mybir.dt.bfloat16
U32 = mybir.dt.uint32
U16 = mybir.dt.uint16
U8 = mybir.dt.uint8
FP8X4 = mybir.dt.float8_e4m3fn_x4
ACT = mybir.ActivationFunctionType

P = 128
PACK = 4
K, ATOMS, EDGES, HIDDEN, OUT_ROWS = 512, 4096, 1024, 512, 128
FLOPS = 2 * (2 * K * HIDDEN * EDGES) + 2 * HIDDEN * OUT_ROWS * EDGES

HALF = EDGES // 2
UNIT = 128
CHUNK = 2 * UNIT
UNITS = EDGES // UNIT
CHUNKS = EDGES // CHUNK
WOVEN_CHUNK = CHUNK * PACK
C_BANKS, F_BANKS, OUT_BANKS = 3, 2, 3
GPSIMD_COLUMNS = (80, 112, 96)
Z_GROUPS = ((0, 1), (2, 3), (4, 5), (6,), (7,))
STORE_ENDS = (2, 6, 7, 8)


def tile_picked_schnet_silu_e_kernel(tc, xT, eT, w1, w3, w2, offs, out):
    nc = tc.nc
    with ExitStack() as ctx:
        keep = ctx.enter_context(tc.tile_pool(name="keep", bufs=1))
        psum = ctx.enter_context(tc.psum_pool(name="psum", bufs=C_BANKS))

        offsets = keep.tile([P, EDGES // 16], U16, name="offsets")
        first_planes = keep.tile([P, 2, ATOMS], F32, name="first_planes")
        planes = {j: keep.tile([P, ATOMS], F32, name=f"plane{j}") for j in range(2, PACK)}
        w1_raw = keep.tile([P, PACK, HIDDEN], F32, align_bytes=64, name="w1_raw")
        w3_raw = keep.tile([P, PACK, HIDDEN], F32, align_bytes=64, name="w3_raw")
        w2_raw = keep.tile([P, PACK, OUT_ROWS], F32, name="w2_raw")
        e_raw = {k: keep.tile([P, PACK, CHUNK], F32, align_bytes=64, name=f"e_raw{k}")[:] for k in (0, 2, 3)}
        e3_first = GPSIMD_COLUMNS[1] * PACK
        relay = keep.tile([P, 2 * WOVEN_CHUNK], BF16, align_bytes=64, name="relay")
        e_raw[1] = relay[:].bitcast(F32).rearrange("p (j n) -> p j n", j=PACK)
        x_rows = xT.rearrange("(p j) n -> p j n", j=PACK)
        e_rows = eT.rearrange("(p j) n -> p j n", j=PACK)

        def load_e(k):
            nc.sync.dma_start(out=e_raw[k], in_=e_rows[:, :, k * CHUNK : (k + 1) * CHUNK])

        nc.sync.dma_start(out=first_planes[:], in_=x_rows[:, 0:2, :])
        nc.sync.dma_start(offsets[:], offs)
        for j in range(2, PACK):
            nc.sync.dma_start(out=planes[j][:], in_=x_rows[:, j, :])
        nc.sync.dma_start(out=w3_raw[:], in_=w3.rearrange("(p j) c -> p j c", j=PACK))
        load_e(0)
        nc.sync.dma_start(out=w1_raw[:], in_=w1.rearrange("(p j) c -> p j c", j=PACK))
        for k in range(1, CHUNKS):
            load_e(k)
        w2_rows = w2.rearrange("(q t r) c -> r q t c", t=PACK, r=2)
        for r in range(2):
            nc.sync.dma_start(out=w2_raw[r:P:2, :, :], in_=w2_rows[r])

        table_warm = keep.tile([P, 1], F32, name="table_warm")
        nc.vector.memset(table_warm[:], 0.0)
        nc.scalar.activation(out=table_warm[:], in_=table_warm[:], func=ACT.Silu)

        x_woven = [keep.tile([P, HALF, PACK], BF16, align_bytes=64, name=f"x_woven{h}") for h in range(2)]
        w1_woven = keep.tile([P, HIDDEN * PACK], BF16, align_bytes=64, name="w1_woven")
        w3_woven = keep.tile([P, HIDDEN * PACK], BF16, align_bytes=64, name="w3_woven")
        e0_woven = keep.tile([P, WOVEN_CHUNK], BF16, align_bytes=64, name="e0_woven")
        e2_first = WOVEN_CHUNK - GPSIMD_COLUMNS[0] * PACK
        e12_woven = keep.tile([P, e2_first + WOVEN_CHUNK], BF16, align_bytes=64, name="e12_woven")
        e_woven = [
            e0_woven[:],
            e12_woven[:, e2_first:],
            e12_woven[:, 0:WOVEN_CHUNK],
            relay[:, e3_first : e3_first + WOVEN_CHUNK],
        ]
        z1_first = (OUT_ROWS - GPSIMD_COLUMNS[2]) * PACK
        w2_z1 = keep.tile([P, z1_first + WOVEN_CHUNK], BF16, align_bytes=64, name="w2_z1")
        w2_woven = w2_z1[:, 0 : OUT_ROWS * PACK]

        def weave(copy, woven, raw, columns):
            pairs = slice(columns.start // 2, columns.stop // 2)
            copy(
                out=woven.rearrange("p (c r j) -> p c j r", r=2, j=PACK)[:, pairs],
                in_=raw.rearrange("p j (c r) -> p c j r", r=2)[:, pairs],
            )

        def weave_dealt(copy, woven, raw, tiles, columns):
            pairs = slice(columns.start // 2, columns.stop // 2)
            copy(
                out=woven[:].rearrange("p (t q r j) -> p q t j r", t=PACK, r=2, j=PACK)[:, pairs, tiles],
                in_=raw[:].rearrange("p j (q t r) -> p q t j r", t=PACK, r=2)[:, pairs, tiles],
            )

        def weave_gpsimd(woven, raw, columns):
            first_pair = (raw.shape[2] - columns) // 2
            nc.gpsimd.tensor_scalar(
                out=woven.rearrange("p (c r j) -> p c j r", r=2, j=PACK)[:, first_pair:],
                in0=raw.rearrange("p j (c r) -> p c j r", r=2)[:, first_pair:],
                scalar1=1.0,
                scalar2=0.0,
                op0=mybir.AluOpType.mult,
                op1=mybir.AluOpType.add,
            )

        def mx_tiles(name, width, codes_tag=""):
            codes = keep.tile([P, width], U32, align_bytes=64, name=f"{name}_codes", tag=codes_tag)
            scales = keep.tile([P, width], U8, align_bytes=64, name=f"{name}_scales")
            return codes, scales

        def quantize(operand, columns, woven):
            codes, scales = operand
            nc.vector.quantize_mx(
                out=codes[:, columns].bitcast(FP8X4),
                scales=scales[:, columns],
                in_=woven[:, columns.start * PACK : columns.stop * PACK],
            )

        def quantize_whole(name, woven, codes_tag=""):
            width = woven.shape[1] // PACK
            operand = mx_tiles(name, width, codes_tag)
            quantize(operand, slice(0, width), woven)
            return operand

        def quantize_weight(name, woven):
            operand = mx_tiles(name, HIDDEN)
            for first in (0, 2 * P):
                quantize(operand, slice(first, first + 2 * P), woven)
            return operand

        def matmul(acc, stationary, stationary_columns, moving, moving_columns):
            nc.tensor.matmul_mx(
                out=acc,
                lhsT=stationary[0][:, stationary_columns].bitcast(FP8X4),
                lhsT_scale=stationary[1][:, stationary_columns],
                rhs=moving[0][:, moving_columns].bitcast(FP8X4),
                rhs_scale=moving[1][:, moving_columns],
                start=True,
                stop=True,
            )

        def product(acc, weight, moving, first):
            for t in range(PACK):
                matmul(acc[:, t, :], weight, slice(t * P, (t + 1) * P), moving, slice(first, first + UNIT))

        x_mx, e_mx, z_mx = {}, {}, {}
        c_acc, f_acc, filters, z_woven = {}, {}, {}, {}

        def f_product(u):
            f_acc[u] = psum.tile([P, PACK, UNIT], F32, name="f_acc", bufs=F_BANKS)
            product(f_acc[u], w3_mx, e_mx[u * UNIT // CHUNK], u * UNIT % CHUNK)

        def c_product(u):
            c_acc[u] = psum.tile([P, PACK, UNIT], F32, name="c_acc", bufs=C_BANKS)
            product(c_acc[u], w1_mx, x_mx[u * UNIT // HALF], u * UNIT % HALF)

        def quantize_e(k):
            e_mx[k] = quantize_whole(f"e{k}", e_woven[k])
            f_product(2 * k)
            f_product(2 * k + 1)

        def quantize_e_unit(u):
            k, first = divmod(u * UNIT, CHUNK)
            quantize(e_mx[k], slice(first, first + UNIT), e_woven[k])
            f_product(u)

        def silu(u):
            if u * UNIT < CHUNK:
                filters[u] = w1_raw[:, u, :].rearrange("p (n t) -> p n t", t=PACK)
            else:
                filters[u] = keep.tile([P, UNIT, PACK], F32, name=f"filter{u}")[:]
            nc.scalar.activation(out=filters[u], in_=f_acc[u][:].rearrange("p t n -> p n t"), func=ACT.Silu)

        def z_place(group):
            if group == Z_GROUPS[-2]:
                return w2_woven.rearrange("p (n t) -> p n t", t=PACK)
            if group == Z_GROUPS[1]:
                return w2_z1[:, z1_first:].rearrange("p (n t) -> p n t", t=PACK)
            if group == Z_GROUPS[0]:
                return relay[:, WOVEN_CHUNK : 2 * WOVEN_CHUNK].rearrange("p (n t) -> p n t", t=PACK)
            return keep.tile([P, len(group) * UNIT, PACK], BF16, align_bytes=64, name=f"z_woven{group[0]}")[:]

        def multiply(u):
            group = [g for g in Z_GROUPS if u in g][0]
            if u == group[0]:
                z_woven[group] = z_place(group)
            first = (u - group[0]) * UNIT
            nc.vector.tensor_tensor(
                out=z_woven[group][:, first : first + UNIT, :],
                in0=c_acc[u][:].rearrange("p t n -> p n t"),
                in1=filters[u],
                op=mybir.AluOpType.mult,
            )
            if u + C_BANKS < UNITS:
                c_product(u + C_BANKS)

        def multiply_pair(k):
            multiply(2 * k)
            multiply(2 * k + 1)
            silu(2 * k + 2)
            silu(2 * k + 3)

        def quantize_z(group, codes_tag=""):
            z_mx[group] = quantize_whole(f"z{group[0]}", z_woven[group].rearrange("p n t -> p (n t)"), codes_tag)

        result = keep.tile([P, EDGES], F32, name="result")

        def project_and_store(group, copy):
            width = len(group) * UNIT
            acc = psum.tile([P, width], F32, name="out_acc", bufs=OUT_BANKS)
            matmul(acc[:], w2_mx, slice(0, OUT_ROWS), z_mx[group], slice(0, width))
            copy(out=result[:, group[0] * UNIT : group[0] * UNIT + width], in_=acc[:])
            if group[-1] + 1 in STORE_ENDS:
                first = ([0] + list(STORE_ENDS))[STORE_ENDS.index(group[-1] + 1)] * UNIT
                last = (group[-1] + 1) * UNIT
                nc.sync.dma_start(out=out[:, first:last], in_=result[:, first:last])

        entries = [offsets[:, h * HALF // 16 : (h + 1) * HALF // 16] for h in range(2)]
        picked = keep.tile([P, 2, EDGES], F32, name="picked")
        picked_late = keep.tile([P, 2, HALF], F32, name="picked_late")
        for j in range(2):
            nc.vector.tensor_copy(picked[:, j, :], first_planes[:, j, :].indirect(offsets[:]))
        for h in range(2):
            nc.scalar.copy(
                out=x_woven[h][:, :, 0:2], in_=picked[:, :, h * HALF : (h + 1) * HALF].rearrange("p j n -> p n j")
            )
        nc.vector.tensor_copy(x_woven[0][:, :, 2], planes[2][:].indirect(entries[0]))
        nc.vector.tensor_copy(picked_late[:, 0, :], planes[2][:].indirect(entries[1]))
        nc.vector.tensor_copy(x_woven[0][:, :, 3], planes[3][:].indirect(entries[0]))
        nc.scalar.activation(picked_late[:, 1, :], planes[3][:].indirect(entries[1]), ACT.Copy)
        nc.scalar.copy(out=x_woven[1][:, :, 2:4], in_=picked_late[:].rearrange("p j n -> p n j"))
        x_mx[0] = quantize_whole("x0", x_woven[0][:].rearrange("p n j -> p (n j)"))

        weave_dealt(nc.vector.tensor_copy, w3_woven, w3_raw, slice(0, 2), slice(0, P))
        weave_dealt(nc.vector.tensor_copy, w3_woven, w3_raw, slice(2, 3), slice(0, P))
        weave_dealt(nc.scalar.copy, w3_woven, w3_raw, slice(3, 4), slice(0, P))
        w3_mx = quantize_weight("w3", w3_woven)
        x_mx[1] = quantize_whole("x1", x_woven[1][:].rearrange("p n j -> p (n j)"), "w3_raw")
        weave(nc.scalar.copy, e_woven[0], e_raw[0], slice(0, CHUNK))
        quantize_e(0)
        weave_dealt(nc.vector.tensor_copy, w1_woven, w1_raw, slice(0, 2), slice(0, P))
        weave_dealt(nc.vector.tensor_copy, w1_woven, w1_raw, slice(2, 4), slice(0, P // 4))
        weave_dealt(nc.scalar.copy, w1_woven, w1_raw, slice(2, 4), slice(P // 4, P))
        w1_mx = quantize_weight("w1", w1_woven)
        for u in range(C_BANKS):
            c_product(u)
        silu(0)
        weave(nc.vector.tensor_copy, e_woven[1], e_raw[1], slice(0, CHUNK))
        silu(1)
        quantize_e(1)

        weave_gpsimd(e_woven[2], e_raw[2], GPSIMD_COLUMNS[0])
        weave(nc.scalar.copy, e_woven[2], e_raw[2], slice(0, UNIT))
        weave(nc.scalar.copy, e_woven[2], e_raw[2], slice(UNIT, CHUNK - GPSIMD_COLUMNS[0]))
        multiply_pair(0)
        e_mx[2] = mx_tiles("e2", CHUNK)
        quantize_e_unit(4)
        quantize_z(Z_GROUPS[0], "e_raw2")
        quantize_e_unit(5)

        weave_gpsimd(e_woven[3], e_raw[3], GPSIMD_COLUMNS[1])
        weave(nc.scalar.copy, e_woven[3], e_raw[3], slice(0, CHUNK - GPSIMD_COLUMNS[1]))
        multiply_pair(1)
        e_mx[3] = mx_tiles("e3", CHUNK)
        quantize_e_unit(6)
        quantize_z(Z_GROUPS[1], "e_raw3")
        quantize_e_unit(7)

        weave_gpsimd(w2_woven, w2_raw[:], GPSIMD_COLUMNS[2])
        weave(nc.scalar.copy, w2_woven, w2_raw[:], slice(0, OUT_ROWS - GPSIMD_COLUMNS[2]))
        multiply_pair(2)
        w2_mx = quantize_whole("w2", w2_woven)
        quantize_z(Z_GROUPS[2])

        for group in Z_GROUPS[-2:]:
            multiply(group[0])
        for group in Z_GROUPS[-2:]:
            quantize_z(group)

        for group in Z_GROUPS[:-1]:
            project_and_store(group, nc.scalar.copy)
        project_and_store(Z_GROUPS[-1], nc.vector.tensor_copy)
